import numpy as np
import ml_dtypes


def mxq(x, axis, fmt="e4m3"):
    dtype, down = {"e4m3": (ml_dtypes.float8_e4m3fn, 7), "e5m2": (ml_dtypes.float8_e5m2, 14)}[fmt]
    v = np.moveaxis(np.asarray(x, np.float32).astype(ml_dtypes.bfloat16).astype(np.float64), axis, -1)
    blocks = v.reshape(v.shape[:-1] + (-1, 32))
    amax = np.abs(blocks).max(-1, keepdims=True)
    byte = np.maximum(np.where(amax > 0, np.frexp(amax)[1] - 1 + 127, 0) - down, 1)
    scale = np.exp2(byte - 127.0)
    codes = (blocks / scale).astype(np.float32).astype(dtype).astype(np.float64)
    return np.moveaxis((codes * scale).reshape(v.shape), -1, axis)


WIDE = False


def mx_kscale(k):
    if not WIDE:
        return np.ones(k)
    levels = np.array([24, -24, 12, -12, 0])
    if k % 512:
        return np.exp2(np.random.permutation(np.resize(levels, k // 32))).repeat(32)
    a = np.empty((k // 512, 16))
    for p in range(k // 512):
        a[p, :8] = np.random.permutation(np.resize(levels, 8))
        for g in range(8):
            far = levels[np.abs(levels - a[p, g]) >= 10]
            a[p, g + 8] = far[np.random.randint(len(far))]
    return np.exp2(a.ravel()).repeat(32)


def f64(x):
    return np.asarray(x).astype(np.float64)


def striped(idx):
    return np.tile(idx.reshape(-1, 16).T, (8, 1)).astype(np.uint16)


def unstriped(offs):
    return offs[:16].T.reshape(-1).astype(np.int64)


E2M1 = np.array([0.0, 0.5, 1.0, 1.5, 2.0, 3.0, 4.0, 6.0, -0.0, -0.5, -1.0, -1.5, -2.0, -3.0, -4.0, -6.0])


def pack_weight(w, fmt):
    k, n = w.shape
    w = f64(np.asarray(w, np.float32).astype(ml_dtypes.bfloat16)).reshape(k // 32, 32, n)
    amax = np.abs(w).max(1)
    if fmt == "e4m3":
        byte = np.frexp(amax)[1] - 1 + 127 - 7
    else:
        mant, ex = np.frexp(amax / 6.0)
        byte = np.where(mant > 0.5, ex, ex - 1) + 127
    byte = np.clip(np.where(amax > 0, byte, 1), 1, 254)
    scaled = (w * np.exp2(127.0 - byte)[:, None, :]).reshape(k, n).astype(np.float32)
    by_word = np.ascontiguousarray(scaled.reshape(k // 512, 128, 4, n).transpose(0, 1, 3, 2))
    if fmt == "e4m3":
        words = by_word.astype(ml_dtypes.float8_e4m3fn).view(np.uint8)
    else:
        c = by_word.astype(ml_dtypes.float4_e2m1fn).view(np.uint8) & 0xF
        words = (c[..., 0::2] | (c[..., 1::2] << 4)).reshape(k // 512, 128, 2 * n)
    return np.ascontiguousarray(words), np.ascontiguousarray(byte.astype(np.uint8).reshape(k // 512, 16, n))


def unpack_weight(words, scales, fmt):
    g, _, n = scales.shape
    words = np.ascontiguousarray(words).reshape(g, 128, n, -1)
    if fmt == "e4m3":
        vals = words.view(ml_dtypes.float8_e4m3fn).astype(np.float64)
    else:
        nib = np.empty((g, 128, n, 4), np.uint8)
        nib[..., 0::2] = words & 0xF
        nib[..., 1::2] = words >> 4
        vals = E2M1[nib]
    vals = vals * np.repeat(np.exp2(scales.astype(np.float64) - 127.0), 8, axis=1)[..., None]
    return vals.transpose(0, 1, 3, 2).reshape(g * 512, n)


def split(x):
    m, e = np.frexp(f64(x))
    hi = np.ldexp(np.trunc(16.0 * m) / 16.0, e)
    return hi, f64(x) - hi


K, L, N, T, J = 512, 1024, 512, 4096, 512


def setup_inputs():
    n = np.random.standard_normal
    s = mx_kscale(K)[:, None]
    s2 = mx_kscale(L)[:, None]
    p_tab = pack_weight(n((K, T)) * s, "e4m3")
    p_w = pack_weight(n((K, N)) / np.sqrt(K) / s, "e2m1")
    return {
        "tab_words": p_tab[0],
        "tab_scales": p_tab[1],
        "w_words": p_w[0],
        "w_scales": p_w[1],
        "x": (n((L, J)) * s2).astype(np.float32),
        "wx": (n((L, N)) / np.sqrt(L) / s2).astype(np.float32),
        "iw0": (np.random.uniform(0.1, 0.6, J)).astype(np.float32),
        "iw1": (np.random.uniform(0.1, 0.6, J)).astype(np.float32),
        "iw2": (np.random.uniform(0.1, 0.6, J)).astype(np.float32),
        "iw3": (np.random.uniform(0.1, 0.6, J)).astype(np.float32),
        "res": (n((N, J))).astype(np.float32),
        "offs": striped(np.concatenate([np.random.permutation(T)[:J] for _ in range(4)])),
    }


def reference(tab_words, tab_scales, w_words, w_scales, x, wx, iw0, iw1, iw2, iw3, res, offs):
    idx = unstriped(offs).reshape(4, J)
    tab_ = unpack_weight(tab_words, tab_scales, "e4m3")[:, idx]
    w_ = unpack_weight(w_words, w_scales, "e2m1")
    a0 = w_.T @ tab_[:, 0]
    a1 = w_.T @ tab_[:, 1]
    a2 = w_.T @ tab_[:, 2]
    a3 = w_.T @ tab_[:, 3]
    x_ = mxq(f64(x), 0, "e4m3")
    wx_hi, wx_lo = split(wx)
    wx_hi_, wx_lo_ = mxq(wx_hi, 0, "e4m3"), mxq(wx_lo, 0, "e4m3")
    ax = wx_hi_.T @ x_ + wx_lo_.T @ x_
    return a0 * f64(iw0)[None, :] + a1 * f64(iw1)[None, :] + a2 * f64(iw2)[None, :] + a3 * f64(iw3)[None, :] + ax + f64(res)

@@ -1,0 +1,193 @@
+from contextlib import ExitStack
+
+import concourse.mybir as mybir
+from concourse.masks import make_identity
+
+K, L, N, T, J, G = 512, 1024, 512, 4096, 512, 4
+FLOPS = 2 * N * J * (G * K + 2 * L)
+
+F32 = mybir.dt.float32
+BF16 = mybir.dt.bfloat16
+I32 = mybir.dt.int32
+U32 = mybir.dt.uint32
+U16 = mybir.dt.uint16
+U8 = mybir.dt.uint8
+FP8X4 = mybir.dt.float8_e4m3fn_x4
+FP4X4 = mybir.dt.float4_e2m1fn_x4
+ALU = mybir.AluOpType
+COPY = mybir.ActivationFunctionType.Copy
+
+P = 128
+PACK = 4
+PASSES = L // (P * PACK)
+JT = J // P
+NT = N // P
+RUN = 4
+HI_MASK = 0xFFF0FFF0 - (1 << 32)
+
+
+def tile_list_interp_hl_res_kernel(
+    tc, tab_words, tab_scales, w_words, w_scales, x, wx, iw0, iw1, iw2, iw3, res, offs, out
+):
+    nc = tc.nc
+
+    def rows_view(ap):
+        return ap.rearrange("p t (c i) -> p c t i", i=RUN)
+
+    def words_view(ap):
+        return ap.rearrange("p (c i) t -> p c t i", i=RUN)
+
+    def load_scale_rows(queue, plane, scales):
+        words = plane[:].bitcast(I32)
+        rows = scales[0].bitcast(I32).rearrange("(q r) c -> r q c", r=4)
+        for r in range(4):
+            queue.dma_start(words[r:P:32, :], rows[r])
+
+    with ExitStack() as ctx:
+        held = ctx.enter_context(tc.tile_pool(name="held", bufs=1))
+        accp = ctx.enter_context(tc.psum_pool(name="acc", bufs=4))
+        sump = ctx.enter_context(tc.psum_pool(name="sums", bufs=1))
+
+        offsets = held.tile([P, G * J // 16], U16, name="offsets")
+        tab_s = held.tile([P, T], U8, name="tab_s", align_bytes=64)
+        tab_w = held.tile([P, T], U32, name="tab_w", align_bytes=64)
+        w_w = held.tile([P, 2 * N], U8, name="w_w", align_bytes=64)
+        w_s = held.tile([P, N], U8, name="w_s", align_bytes=64)
+        ident = held.tile([P, P], F32, name="ident")
+        iw_rows = held.tile([P, P], F32, name="iw_rows")
+        iw_cols = held.tile([P, G * JT], F32, name="iw_cols")
+
+        HALF = N // 2
+
+        def load_chunk(src, h, a, name, tag):
+            raw = held.tile([P, PACK, HALF], F32, name=name, tag=tag, align_bytes=64)
+            rows = src[a * P * PACK : (a + 1) * P * PACK, h * HALF : (h + 1) * HALF]
+            nc.sync.dma_start(raw[:], rows.rearrange("(p t) c -> p t c", t=PACK))
+            return raw
+
+        def grouped(name, tag):
+            return held.tile([P, HALF, PACK], BF16, name=name, tag=tag, align_bytes=64)
+
+        def quantise(src, name):
+            codes = held.tile([P, HALF], U32, name=name + "_c", align_bytes=64)
+            scales = held.tile([P, HALF], U8, name=name + "_s", align_bytes=64)
+            nc.vector.quantize_mx(
+                out=codes[:].bitcast(FP8X4), scales=scales[:], in_=src[:].rearrange("p c t -> p (c t)")
+            )
+            return codes, scales
+
+        def as_pairs(tile):
+            return tile[:].rearrange("p c t -> p (c t)").bitcast(I32)
+
+        def split(raw, name, copy, hi_tag):
+            upper = grouped("upper" + name, "upper" + name)
+            tops = raw[:].bitcast(BF16).rearrange("p t (c two) -> p t c two", two=2)[:, :, :, 1]
+            copy(words_view(upper[:]), rows_view(tops))
+            hi, lo = grouped("hi" + name, hi_tag), grouped("lo" + name, "lo" + name)
+            nc.vector.tensor_scalar(as_pairs(hi), as_pairs(upper), HI_MASK, None, ALU.bitwise_and)
+            nc.vector.tensor_tensor(words_view(lo[:]), rows_view(raw[:]), words_view(hi[:]), ALU.subtract)
+            return [quantise(hi, "q_hi" + name), quantise(lo, "q_lo" + name)]
+
+        def cast(raw, name, copy, tag):
+            xb = grouped("xb" + name, tag)
+            copy(words_view(xb[:]), rows_view(raw[:]))
+            return quantise(xb, "q_x" + name)
+
+        nc.gpsimd.memset(iw_rows[:], 0.0)
+        nc.vector.memset(tab_s[:].bitcast(I32), 0)
+        nc.vector.memset(w_s[:].bitcast(I32), 0)
+        wx_raw, x_raw, q_wx, q_x = {}, {}, {}, {}
+        wx_raw[0, 0] = load_chunk(wx, 0, 0, "wx00", "wx00")
+        nc.sync.dma_start(offsets[:], offs)
+        nc.sync.dma_start(w_w[:].bitcast(I32), w_words[0].bitcast(I32))
+        for g, iw in enumerate((iw0, iw1, iw2, iw3)):
+            nc.scalar.dma_start(iw_rows[g * JT : (g + 1) * JT, :], iw.rearrange("(jt p) -> jt p", p=P))
+        nc.sync.dma_start(
+            tab_w[:].bitcast(I32), tab_words[0].rearrange("p t i -> p (t i)").bitcast(I32)
+        )
+        load_scale_rows(nc.scalar, tab_s, tab_scales)
+        wx_raw[0, 1] = load_chunk(wx, 0, 1, "wx01", "wx01")
+        x_raw[0, 0] = load_chunk(x, 0, 0, "x00", "x00")
+        load_scale_rows(nc.scalar, w_s, w_scales)
+
+        make_identity(nc, ident[:])
+        iw_ps = accp.tile([P, N], F32, name="acc")
+        nc.tensor.transpose(iw_ps[:, 0:P], iw_rows[:], ident[:])
+        nc.scalar.activation(iw_cols[:], iw_ps[:, 0 : G * JT], COPY)
+
+        sums = [sump.tile([P, NT, P], F32, name=f"sum{jt}") for jt in range(JT)]
+        parts = {}
+
+        def project(g):
+            picks = offsets[:, g * J // 16 : (g + 1) * J // 16]
+            got_w = held.tile([P, J], U32, name=f"got_w{g}", align_bytes=64)
+            got_s = held.tile([P, J], U8, name=f"got_s{g}", align_bytes=64)
+            nc.vector.tensor_copy(got_w[:], tab_w[:].indirect(picks))
+            nc.vector.tensor_copy(got_s[:], tab_s[:].indirect(picks))
+            for jt in range(JT):
+                acc = accp.tile([P, N], F32, name="acc")
+                nc.tensor.matmul_mx(
+                    acc[:], lhsT=got_w[:, jt * P : (jt + 1) * P].bitcast(FP8X4),
+                    lhsT_scale=got_s[:, jt * P : (jt + 1) * P],
+                    rhs=w_w[:].bitcast(FP4X4), rhs_scale=w_s[:], start=True, stop=True,
+                )
+                part = held.tile([P, N], F32, name=f"part{g}_{jt}")
+                nc.scalar.activation(part[:], acc[:], COPY, scale=iw_cols[:, g * JT + jt : g * JT + jt + 1])
+                parts[g, jt] = part
+
+        def add_transposed(g):
+            for jt in range(JT):
+                for nt in range(NT):
+                    nc.tensor.matmul(
+                        sums[jt][:, nt, :], parts[g, jt][:, nt * P : (nt + 1) * P], ident[:],
+                        start=g == 0 and nt == 0, stop=g == G - 1 and nt == NT - 1, is_transpose=True,
+                    )
+
+        on_vector, on_scalar = nc.vector.tensor_copy, nc.scalar.copy
+        q_wx[0, 0] = split(wx_raw[0, 0], "00", on_vector, "hi00")
+        x_raw[0, 1] = load_chunk(x, 0, 1, "x01", "upper00")
+        wx_raw[1, 0] = load_chunk(wx, 1, 0, "wx10", "wx00")
+        wx_raw[1, 1] = load_chunk(wx, 1, 1, "wx11", "hi00")
+        project(0)
+        project(1)
+        add_transposed(0)
+        q_wx[0, 1] = split(wx_raw[0, 1], "01", on_scalar, "got_w0")
+        x_raw[1, 0] = load_chunk(x, 1, 0, "x10", "upper01")
+        x_raw[1, 1] = load_chunk(x, 1, 1, "x11", "wx01")
+        res_sb = held.tile([P, NT, J], F32, name="res_sb", tag="got_w1", align_bytes=64)
+        nc.sync.dma_start(res_sb[:], res.rearrange("(nt p) j -> p nt j", p=P))
+        project(2)
+        add_transposed(1)
+        project(3)
+        add_transposed(2)
+        add_transposed(3)
+        q_x[0, 0] = cast(x_raw[0, 0], "00", on_vector, "got_s1")
+        q_wx[1, 0] = split(wx_raw[1, 0], "10", on_vector, "got_s2")
+        q_x[0, 1] = cast(x_raw[0, 1], "01", on_scalar, "got_s0")
+        q_wx[1, 1] = split(wx_raw[1, 1], "11", on_scalar, "got_w2")
+        q_x[1, 0] = cast(x_raw[1, 0], "10", on_scalar, "xb10")
+        q_x[1, 1] = cast(x_raw[1, 1], "11", on_scalar, "xb11")
+
+        base = held.tile([P, NT, J], F32, name="base")
+        for jt in range(JT):
+            cols = slice(jt * P, (jt + 1) * P)
+            nc.vector.tensor_tensor(base[:, :, cols], sums[jt][:], res_sb[:, :, cols], ALU.add)
+
+        out_v = out.rearrange("(nt p) j -> p nt j", p=P)
+        for jh in range(2):
+            cols = slice(jh * HALF, (jh + 1) * HALF)
+            for nh in range(2):
+                acc = accp.tile([P, 2, HALF], F32, name="acc")
+                steps = [(a, q) for a in range(PASSES) for q in q_wx[nh, a]]
+                for i in range(2):
+                    for s, (a, q) in enumerate(steps):
+                        nc.tensor.matmul_mx(
+                            acc[:, i, :], lhsT=q[0][:, i * P : (i + 1) * P].bitcast(FP8X4),
+                            lhsT_scale=q[1][:, i * P : (i + 1) * P],
+                            rhs=q_x[jh, a][0][:].bitcast(FP8X4), rhs_scale=q_x[jh, a][1][:],
+                            start=s == 0, stop=s == len(steps) - 1,
+                        )
+                done = held.tile([P, 2, HALF], F32, name=f"done{jh}{nh}")
+                rows = slice(2 * nh, 2 * nh + 2)
+                nc.vector.tensor_tensor(done[:], acc[:], base[:, rows, cols], ALU.add)
+                nc.sync.dma_start(out_v[:, rows, cols], done[:])

@@ -30,6 +30,7 @@ def tile_list_interp_hl_res_kernel(
     tc, tab_words, tab_scales, w_words, w_scales, x, wx, iw0, iw1, iw2, iw3, res, offs, out
 ):
     nc = tc.nc
+    HALF = N // 2
 
     def rows_view(ap):
         return ap.rearrange("p t (c i) -> p c t i", i=RUN)
@@ -37,157 +38,198 @@ def tile_list_interp_hl_res_kernel(
     def words_view(ap):
         return ap.rearrange("p (c i) t -> p c t i", i=RUN)
 
-    def load_scale_rows(queue, plane, scales):
+    def load_scale_rows(plane, scales):
         words = plane[:].bitcast(I32)
         rows = scales[0].bitcast(I32).rearrange("(q r) c -> r q c", r=4)
         for r in range(4):
-            queue.dma_start(words[r:P:32, :], rows[r])
+            nc.sync.dma_start(words[r:P:32, :], rows[r])
 
     with ExitStack() as ctx:
         held = ctx.enter_context(tc.tile_pool(name="held", bufs=1))
-        accp = ctx.enter_context(tc.psum_pool(name="acc", bufs=4))
-        sump = ctx.enter_context(tc.psum_pool(name="sums", bufs=1))
+        psum = ctx.enter_context(tc.psum_pool(name="psum", bufs=1))
+
+        def sb(shape, dtype, name, tag=None):
+            return held.tile(shape, dtype, name=name, tag=tag or name, align_bytes=64)
 
         offsets = held.tile([P, G * J // 16], U16, name="offsets")
-        tab_s = held.tile([P, T], U8, name="tab_s", align_bytes=64)
-        tab_w = held.tile([P, T], U32, name="tab_w", align_bytes=64)
-        w_w = held.tile([P, 2 * N], U8, name="w_w", align_bytes=64)
-        w_s = held.tile([P, N], U8, name="w_s", align_bytes=64)
-        ident = held.tile([P, P], F32, name="ident")
-        iw_rows = held.tile([P, P], F32, name="iw_rows")
-        iw_cols = held.tile([P, G * JT], F32, name="iw_cols")
+        tab_s = sb([P, T], U8, "tab_s")
+        tab_w = sb([P, T], U32, "tab_w")
+        w_w = sb([P, 2 * N], U8, "w_w")
+        w_s = sb([P, N], U8, "w_s")
+        ident = sb([P, P], F32, "ident")
+        iw_rows = [sb([P, P], F32, f"iw_rows{h}") for h in range(2)]
+        iw_cols = [sb([P, 2 * JT], F32, f"iw_cols{h}") for h in range(2)]
 
-        HALF = N // 2
+        def bank(b, name):
+            return psum.tile([P, N], F32, name=name, tag=f"bank{b}")
 
-        def load_chunk(src, h, a, name, tag):
-            raw = held.tile([P, PACK, HALF], F32, name=name, tag=tag, align_bytes=64)
-            rows = src[a * P * PACK : (a + 1) * P * PACK, h * HALF : (h + 1) * HALF]
-            nc.sync.dma_start(raw[:], rows.rearrange("(p t) c -> p t c", t=PACK))
+        def load_piece(src, a, c0, width, name):
+            raw = sb([P, PACK * width], F32, name)[:].rearrange("p (t c) -> p t c", t=PACK)
+            rows = src[a * P * PACK : (a + 1) * P * PACK, c0 : c0 + width]
+            nc.sync.dma_start(raw, rows.rearrange("(p t) c -> p t c", t=PACK))
             return raw
 
-        def grouped(name, tag):
-            return held.tile([P, HALF, PACK], BF16, name=name, tag=tag, align_bytes=64)
-
-        def quantise(src, name):
-            codes = held.tile([P, HALF], U32, name=name + "_c", align_bytes=64)
-            scales = held.tile([P, HALF], U8, name=name + "_s", align_bytes=64)
-            nc.vector.quantize_mx(
-                out=codes[:].bitcast(FP8X4), scales=scales[:], in_=src[:].rearrange("p c t -> p (c t)")
-            )
+        def quantise(src, name, width):
+            codes = sb([P, width], U32, name + "_c")
+            scales = sb([P, width], U8, name + "_s")
+            nc.vector.quantize_mx(out=codes[:].bitcast(FP8X4), scales=scales[:], in_=src)
             return codes, scales
 
-        def as_pairs(tile):
-            return tile[:].rearrange("p c t -> p (c t)").bitcast(I32)
+        def flat(ap):
+            return ap.rearrange("p c t -> p (c t)")
 
-        def split(raw, name, copy, hi_tag):
-            upper = grouped("upper" + name, "upper" + name)
-            tops = raw[:].bitcast(BF16).rearrange("p t (c two) -> p t c two", two=2)[:, :, :, 1]
-            copy(words_view(upper[:]), rows_view(tops))
-            hi, lo = grouped("hi" + name, hi_tag), grouped("lo" + name, "lo" + name)
-            nc.vector.tensor_scalar(as_pairs(hi), as_pairs(upper), HI_MASK, None, ALU.bitwise_and)
-            nc.vector.tensor_tensor(words_view(lo[:]), rows_view(raw[:]), words_view(hi[:]), ALU.subtract)
-            return [quantise(hi, "q_hi" + name), quantise(lo, "q_lo" + name)]
+        def upper_halves(raw, dst, copy):
+            tops = raw.bitcast(BF16).rearrange("p t (c two) -> p t c two", two=2)[:, :, :, 1]
+            copy(words_view(dst), rows_view(tops))
 
-        def cast(raw, name, copy, tag):
-            xb = grouped("xb" + name, tag)
-            copy(words_view(xb[:]), rows_view(raw[:]))
-            return quantise(xb, "q_x" + name)
+        def split(raws, upper, name, tag=None):
+            width = HALF * len(raws)
+            both = sb([P, 2 * width, PACK], BF16, "hi_lo" + name, tag)
+            nc.vector.tensor_scalar(
+                flat(both[:, 0:width, :]).bitcast(I32), flat(upper).bitcast(I32), HI_MASK, None, ALU.bitwise_and
+            )
+            for i, raw in enumerate(raws):
+                hi = both[:, i * HALF : (i + 1) * HALF, :]
+                lo = both[:, width + i * HALF : width + (i + 1) * HALF, :]
+                nc.vector.tensor_tensor(words_view(lo), rows_view(raw), words_view(hi), ALU.subtract)
+            codes, scales = quantise(flat(both[:]), "q" + name, 2 * width)
+            return [
+                [(codes, scales, part * width + i * HALF) for part in range(2)] for i in range(len(raws))
+            ]
 
-        nc.gpsimd.memset(iw_rows[:], 0.0)
-        nc.vector.memset(tab_s[:].bitcast(I32), 0)
-        nc.vector.memset(w_s[:].bitcast(I32), 0)
+        def cast(raw, dst, copy):
+            copy(words_view(dst), rows_view(raw))
+
+        def load_weight(g):
+            rows = iw_rows[g // 2][(g % 2) * JT : (g % 2 + 1) * JT, :]
+            nc.sync.dma_start(rows, (iw0, iw1, iw2, iw3)[g].rearrange("(jt p) -> jt p", p=P))
+
         wx_raw, x_raw, q_wx, q_x = {}, {}, {}, {}
-        wx_raw[0, 0] = load_chunk(wx, 0, 0, "wx00", "wx00")
+        nc.gpsimd.memset(tab_s[:].bitcast(I32)[:, 0 : T // 8], 0)
+        nc.vector.memset(iw_rows[0][:], 0.0)
+        nc.vector.memset(tab_s[:].bitcast(I32)[:, T // 8 : T // 4], 0)
+        nc.vector.memset(w_s[:].bitcast(I32), 0)
+        nc.vector.memset(iw_rows[1][:], 0.0)
+        make_identity(nc, ident[:])
         nc.sync.dma_start(offsets[:], offs)
         nc.sync.dma_start(w_w[:].bitcast(I32), w_words[0].bitcast(I32))
-        for g, iw in enumerate((iw0, iw1, iw2, iw3)):
-            nc.scalar.dma_start(iw_rows[g * JT : (g + 1) * JT, :], iw.rearrange("(jt p) -> jt p", p=P))
-        nc.sync.dma_start(
-            tab_w[:].bitcast(I32), tab_words[0].rearrange("p t i -> p (t i)").bitcast(I32)
-        )
-        load_scale_rows(nc.scalar, tab_s, tab_scales)
-        wx_raw[0, 1] = load_chunk(wx, 0, 1, "wx01", "wx01")
-        x_raw[0, 0] = load_chunk(x, 0, 0, "x00", "x00")
-        load_scale_rows(nc.scalar, w_s, w_scales)
+        load_weight(0)
+        load_scale_rows(tab_s, tab_scales)
+        res_sb = sb([P, NT, J], F32, "res_sb")
 
-        make_identity(nc, ident[:])
-        iw_ps = accp.tile([P, N], F32, name="acc")
-        nc.tensor.transpose(iw_ps[:, 0:P], iw_rows[:], ident[:])
-        nc.scalar.activation(iw_cols[:], iw_ps[:, 0 : G * JT], COPY)
+        def load_table():
+            nc.sync.dma_start(
+                tab_w[:].bitcast(I32), tab_words[0].rearrange("p t i -> p (t i)").bitcast(I32)
+            )
 
-        sums = [sump.tile([P, NT, P], F32, name=f"sum{jt}") for jt in range(JT)]
-        parts = {}
+        def load_res():
+            nc.sync.dma_start(res_sb[:], res.rearrange("(nt p) j -> p nt j", p=P))
 
-        def project(g):
+        def load_wx(a):
+            whole = load_piece(wx, a, 0, N, f"wx{a}")
+            wx_raw[0, a], wx_raw[1, a] = whole[:, :, 0:HALF], whole[:, :, HALF:N]
+
+        wx_raw[0, 0] = load_piece(wx, 0, 0, HALF, "wx00")
+        load_table()
+        load_weight(1)
+        load_scale_rows(w_s, w_scales)
+        wx_raw[1, 0] = load_piece(wx, 0, HALF, HALF, "wx10")
+        x_raw[0] = load_piece(x, 0, 0, J, "x0")
+        load_weight(2)
+        load_weight(3)
+        load_wx(1)
+        x_raw[1] = load_piece(x, 1, 0, J, "x1")
+        load_res()
+
+        def turn_weights(h, b):
+            iw_ps = bank(b, f"iw_ps{h}")
+            nc.tensor.transpose(iw_ps[:, 0:P], iw_rows[h][:], ident[:])
+            nc.scalar.activation(iw_cols[h][:], iw_ps[:, 0 : 2 * JT], COPY)
+
+        sums = [psum.tile([P, J], F32, name=f"sum{nt}") for nt in range(NT)]
+        got_s = sb([P, G * J], U8, "got_s")
+        got_w = {}
+
+        def gather_words(g, tag=None):
+            got_w[g] = sb([P, J], U32, f"got_w{g}", tag)
             picks = offsets[:, g * J // 16 : (g + 1) * J // 16]
-            got_w = held.tile([P, J], U32, name=f"got_w{g}", align_bytes=64)
-            got_s = held.tile([P, J], U8, name=f"got_s{g}", align_bytes=64)
-            nc.vector.tensor_copy(got_w[:], tab_w[:].indirect(picks))
-            nc.vector.tensor_copy(got_s[:], tab_s[:].indirect(picks))
-            for jt in range(JT):
-                acc = accp.tile([P, N], F32, name="acc")
-                nc.tensor.matmul_mx(
-                    acc[:], lhsT=got_w[:, jt * P : (jt + 1) * P].bitcast(FP8X4),
-                    lhsT_scale=got_s[:, jt * P : (jt + 1) * P],
-                    rhs=w_w[:].bitcast(FP4X4), rhs_scale=w_s[:], start=True, stop=True,
-                )
-                part = held.tile([P, N], F32, name=f"part{g}_{jt}")
-                nc.scalar.activation(part[:], acc[:], COPY, scale=iw_cols[:, g * JT + jt : g * JT + jt + 1])
-                parts[g, jt] = part
+            nc.vector.tensor_copy(got_w[g][:], tab_w[:].indirect(picks))
 
-        def add_transposed(g):
-            for jt in range(JT):
+        waiting = []
+
+        def add_transposed():
+            pair = waiting[0:2]
+            for item in pair:
+                waiting.remove(item)
+            for g, jt, part in reversed(pair):
                 for nt in range(NT):
                     nc.tensor.matmul(
-                        sums[jt][:, nt, :], parts[g, jt][:, nt * P : (nt + 1) * P], ident[:],
-                        start=g == 0 and nt == 0, stop=g == G - 1 and nt == NT - 1, is_transpose=True,
+                        sums[nt][:, jt * P : (jt + 1) * P], part[:, nt * P : (nt + 1) * P], ident[:],
+                        start=(g, jt) == (0, 1), stop=(g, jt) == (G - 1, JT - 2), is_transpose=True,
                     )
 
+        def project(g, tiles):
+            for jt in tiles:
+                acc = bank(jt, f"acc{g}_{jt}")
+                nc.tensor.matmul_mx(
+                    acc[:], lhsT=got_w[g][:, jt * P : (jt + 1) * P].bitcast(FP8X4),
+                    lhsT_scale=got_s[:, g * J + jt * P : g * J + (jt + 1) * P],
+                    rhs=w_w[:].bitcast(FP4X4), rhs_scale=w_s[:], start=True, stop=True,
+                )
+                part = sb([P, N], F32, f"part{g}_{jt}")
+                col = (g % 2) * JT + jt
+                nc.scalar.activation(part[:], acc[:], COPY, scale=iw_cols[g // 2][:, col : col + 1])
+                waiting.append((g, jt, part))
+                if len(waiting) == JT + 2:
+                    add_transposed()
+
+        def skip_pass(acc, nt, a):
+            for s, (codes, scales, first) in enumerate(q_wx[nt // 2, a]):
+                cols = slice(first + (nt % 2) * P, first + (nt % 2 + 1) * P)
+                nc.tensor.matmul_mx(
+                    acc[:], lhsT=codes[:, cols].bitcast(FP8X4), lhsT_scale=scales[:, cols],
+                    rhs=q_x[a][0][:].bitcast(FP8X4), rhs_scale=q_x[a][1][:],
+                    start=a == 0 and s == 0, stop=a == PASSES - 1 and s == 1,
+                )
+
         on_vector, on_scalar = nc.vector.tensor_copy, nc.scalar.copy
-        q_wx[0, 0] = split(wx_raw[0, 0], "00", on_vector, "hi00")
-        x_raw[0, 1] = load_chunk(x, 0, 1, "x01", "upper00")
-        wx_raw[1, 0] = load_chunk(wx, 1, 0, "wx10", "wx00")
-        wx_raw[1, 1] = load_chunk(wx, 1, 1, "wx11", "hi00")
-        project(0)
-        project(1)
-        add_transposed(0)
-        q_wx[0, 1] = split(wx_raw[0, 1], "01", on_scalar, "got_w0")
-        x_raw[1, 0] = load_chunk(x, 1, 0, "x10", "upper01")
-        x_raw[1, 1] = load_chunk(x, 1, 1, "x11", "wx01")
-        res_sb = held.tile([P, NT, J], F32, name="res_sb", tag="got_w1", align_bytes=64)
-        nc.sync.dma_start(res_sb[:], res.rearrange("(nt p) j -> p nt j", p=P))
-        project(2)
-        add_transposed(1)
-        project(3)
-        add_transposed(2)
-        add_transposed(3)
-        q_x[0, 0] = cast(x_raw[0, 0], "00", on_vector, "got_s1")
-        q_wx[1, 0] = split(wx_raw[1, 0], "10", on_vector, "got_s2")
-        q_x[0, 1] = cast(x_raw[0, 1], "01", on_scalar, "got_s0")
-        q_wx[1, 1] = split(wx_raw[1, 1], "11", on_scalar, "got_w2")
-        q_x[1, 0] = cast(x_raw[1, 0], "10", on_scalar, "xb10")
-        q_x[1, 1] = cast(x_raw[1, 1], "11", on_scalar, "xb11")
-
-        base = held.tile([P, NT, J], F32, name="base")
-        for jt in range(JT):
-            cols = slice(jt * P, (jt + 1) * P)
-            nc.vector.tensor_tensor(base[:, :, cols], sums[jt][:], res_sb[:, :, cols], ALU.add)
-
-        out_v = out.rearrange("(nt p) j -> p nt j", p=P)
-        for jh in range(2):
-            cols = slice(jh * HALF, (jh + 1) * HALF)
-            for nh in range(2):
-                acc = accp.tile([P, 2, HALF], F32, name="acc")
-                steps = [(a, q) for a in range(PASSES) for q in q_wx[nh, a]]
-                for i in range(2):
-                    for s, (a, q) in enumerate(steps):
-                        nc.tensor.matmul_mx(
-                            acc[:, i, :], lhsT=q[0][:, i * P : (i + 1) * P].bitcast(FP8X4),
-                            lhsT_scale=q[1][:, i * P : (i + 1) * P],
-                            rhs=q_x[jh, a][0][:].bitcast(FP8X4), rhs_scale=q_x[jh, a][1][:],
-                            start=s == 0, stop=s == len(steps) - 1,
-                        )
-                done = held.tile([P, 2, HALF], F32, name=f"done{jh}{nh}")
-                rows = slice(2 * nh, 2 * nh + 2)
-                nc.vector.tensor_tensor(done[:], acc[:], base[:, rows, cols], ALU.add)
-                nc.sync.dma_start(out_v[:, rows, cols], done[:])
+        nc.vector.tensor_copy(got_s[:], tab_s[:].indirect(offsets[:]))
+        upper0 = sb([P, N, PACK], BF16, "upper0")
+        upper_halves(wx_raw[0, 0], upper0[:, 0:HALF, :], on_scalar)
+        turn_weights(0, 0)
+        gather_words(0, "tab_s")
+        for g in range(1, G):
+            gather_words(g)
+        upper_halves(wx_raw[1, 0], upper0[:, HALF:N, :], on_scalar)
+        project(0, range(JT))
+        turn_weights(1, 0)
+        q_wx[0, 0], q_wx[1, 0] = split((wx_raw[0, 0], wx_raw[1, 0]), upper0[:], "0", "tab_w")
+        xb0 = sb([P, J, PACK], BF16, "xb0", "upper0")
+        cast(x_raw[0], xb0[:], on_vector)
+        q_x[0] = quantise(flat(xb0[:]), "q_x0", J)
+        project(1, (0, 1, 2))
+        upper01 = sb([P, HALF, PACK], BF16, "upper01", "part0_1")
+        upper_halves(wx_raw[0, 1], upper01[:], on_scalar)
+        project(1, (3,))
+        project(2, (0, 1, 2))
+        upper11 = sb([P, HALF, PACK], BF16, "upper11", "part1_1")
+        upper_halves(wx_raw[1, 1], upper11[:], on_scalar)
+        [q_wx[0, 1]] = split((wx_raw[0, 1],), upper01[:], "01", "upper0")
+        xb1 = sb([P, J, PACK], BF16, "xb1", "part0_1")
+        cast(x_raw[1], xb1[:], on_vector)
+        q_x[1] = quantise(flat(xb1[:]), "q_x1", J)
+        [q_wx[1, 1]] = split((wx_raw[1, 1],), upper11[:], "11", "part0_1")
+        project(2, (3,))
+        project(3, range(JT))
+        for pair in range(JT // 2):
+            add_transposed()
+        base = [sb([P, J], F32, f"base{nt}") for nt in range(NT)]
+        for nt in range(NT):
+            nc.vector.tensor_tensor(base[nt][:], sums[nt][:], res_sb[:, nt, :], ALU.add)
+        for nt in range(NT):
+            skip = bank(nt, f"skip{nt}")
+            for a in range(PASSES):
+                skip_pass(skip, nt, a)
+            done = sb([P, J], F32, f"done{nt}")
+            nc.vector.tensor_tensor(done[:], skip[:], base[nt][:], ALU.add)
+            nc.sync.dma_start(out[nt * P : (nt + 1) * P, :], done[:])

@@ -69,8 +69,8 @@ def tile_list_interp_hl_res_kernel(
             nc.sync.dma_start(raw, rows.rearrange("(p t) c -> p t c", t=PACK))
             return raw
 
-        def quantise(src, name, width):
-            codes = sb([P, width], U32, name + "_c")
+        def quantise(src, name, width, tag=None):
+            codes = sb([P, width], U32, name + "_c", tag)
             scales = sb([P, width], U8, name + "_s")
             nc.vector.quantize_mx(out=codes[:].bitcast(FP8X4), scales=scales[:], in_=src)
             return codes, scales
@@ -82,19 +82,22 @@ def tile_list_interp_hl_res_kernel(
             tops = raw.bitcast(BF16).rearrange("p t (c two) -> p t c two", two=2)[:, :, :, 1]
             copy(words_view(dst), rows_view(tops))
 
-        def split(raws, upper, name, tag=None):
-            width = HALF * len(raws)
+        def truncate(upper, width, name, tag=None):
             both = sb([P, 2 * width, PACK], BF16, "hi_lo" + name, tag)
             nc.vector.tensor_scalar(
                 flat(both[:, 0:width, :]).bitcast(I32), flat(upper).bitcast(I32), HI_MASK, None, ALU.bitwise_and
             )
-            for i, raw in enumerate(raws):
-                hi = both[:, i * HALF : (i + 1) * HALF, :]
-                lo = both[:, width + i * HALF : width + (i + 1) * HALF, :]
-                nc.vector.tensor_tensor(words_view(lo), rows_view(raw), words_view(hi), ALU.subtract)
-            codes, scales = quantise(flat(both[:]), "q" + name, 2 * width)
+            return both
+
+        def subtract(raw, both, width, i):
+            hi = both[:, i * HALF : (i + 1) * HALF, :]
+            lo = both[:, width + i * HALF : width + (i + 1) * HALF, :]
+            nc.vector.tensor_tensor(words_view(lo), rows_view(raw), words_view(hi), ALU.subtract)
+
+        def quantise_split(both, width, name, tag=None):
+            codes, scales = quantise(flat(both[:]), "q" + name, 2 * width, tag)
             return [
-                [(codes, scales, part * width + i * HALF) for part in range(2)] for i in range(len(raws))
+                [(codes, scales, part * width + i * HALF) for part in range(2)] for i in range(width // HALF)
             ]
 
         def cast(raw, dst, copy):
@@ -104,9 +107,9 @@ def tile_list_interp_hl_res_kernel(
             rows = iw_rows[g // 2][(g % 2) * JT : (g % 2 + 1) * JT, :]
             nc.sync.dma_start(rows, (iw0, iw1, iw2, iw3)[g].rearrange("(jt p) -> jt p", p=P))
 
-        wx_raw, x_raw, q_wx, q_x = {}, {}, {}, {}
+        wx_raw, wx_whole, x_raw, q_wx, q_x = {}, {}, {}, {}, {}
+        nc.gpsimd.memset(iw_rows[0][:], 0.0)
         nc.gpsimd.memset(tab_s[:].bitcast(I32)[:, 0 : T // 8], 0)
-        nc.vector.memset(iw_rows[0][:], 0.0)
         nc.vector.memset(tab_s[:].bitcast(I32)[:, T // 8 : T // 4], 0)
         nc.vector.memset(w_s[:].bitcast(I32), 0)
         nc.vector.memset(iw_rows[1][:], 0.0)
@@ -127,16 +130,16 @@ def tile_list_interp_hl_res_kernel(
 
         def load_wx(a):
             whole = load_piece(wx, a, 0, N, f"wx{a}")
+            wx_whole[a] = whole
             wx_raw[0, a], wx_raw[1, a] = whole[:, :, 0:HALF], whole[:, :, HALF:N]
 
-        wx_raw[0, 0] = load_piece(wx, 0, 0, HALF, "wx00")
         load_table()
         load_weight(1)
+        load_wx(0)
         load_scale_rows(w_s, w_scales)
-        wx_raw[1, 0] = load_piece(wx, 0, HALF, HALF, "wx10")
-        x_raw[0] = load_piece(x, 0, 0, J, "x0")
         load_weight(2)
         load_weight(3)
+        x_raw[0] = load_piece(x, 0, 0, J, "x0")
         load_wx(1)
         x_raw[1] = load_piece(x, 1, 0, J, "x1")
         load_res()
@@ -194,42 +197,57 @@ def tile_list_interp_hl_res_kernel(
 
         on_vector, on_scalar = nc.vector.tensor_copy, nc.scalar.copy
         nc.vector.tensor_copy(got_s[:], tab_s[:].indirect(offsets[:]))
-        upper0 = sb([P, N, PACK], BF16, "upper0")
-        upper_halves(wx_raw[0, 0], upper0[:, 0:HALF, :], on_scalar)
         turn_weights(0, 0)
         gather_words(0, "tab_s")
-        for g in range(1, G):
+        for g in range(1, G - 1):
             gather_words(g)
-        upper_halves(wx_raw[1, 0], upper0[:, HALF:N, :], on_scalar)
+        upper0 = sb([P, N, PACK], BF16, "upper0")
+        upper_halves(wx_whole[0], upper0[:], on_scalar)
         project(0, range(JT))
         turn_weights(1, 0)
-        q_wx[0, 0], q_wx[1, 0] = split((wx_raw[0, 0], wx_raw[1, 0]), upper0[:], "0", "tab_w")
-        xb0 = sb([P, J, PACK], BF16, "xb0", "upper0")
+        both0 = truncate(upper0[:], N, "0")
+        gather_words(G - 1, "upper0")
+        subtract(wx_raw[0, 0], both0, N, 0)
+        xb0 = sb([P, J, PACK], BF16, "xb0")
         cast(x_raw[0], xb0[:], on_vector)
-        q_x[0] = quantise(flat(xb0[:]), "q_x0", J)
-        project(1, (0, 1, 2))
+        subtract(wx_raw[1, 0], both0, N, 1)
+        q_x[0] = quantise(flat(xb0[:]), "q_x0", J, "wx0")
+        q_wx[0, 0], q_wx[1, 0] = quantise_split(both0, N, "0", "x0")
+        project(1, range(JT))
+        q_x[1] = sb([P, J], U32, "q_x1_c"), sb([P, J], U8, "q_x1_s")
+
+        def last_pass(h, upper, tag):
+            cols = slice(h * HALF, (h + 1) * HALF)
+            both = truncate(upper[:], HALF, f"{h}1", tag)
+            xb = sb([P, HALF, PACK], BF16, f"xb1{h}", f"part{h}_1")
+            cast(x_raw[1][:, :, cols], xb[:], on_vector)
+            subtract(wx_raw[h, 1], both, HALF, 0)
+            nc.vector.quantize_mx(out=q_x[1][0][:, cols].bitcast(FP8X4), scales=q_x[1][1][:, cols], in_=flat(xb[:]))
+            [q_wx[h, 1]] = quantise_split(both, HALF, f"{h}1")
+
         upper01 = sb([P, HALF, PACK], BF16, "upper01", "part0_1")
         upper_halves(wx_raw[0, 1], upper01[:], on_scalar)
-        project(1, (3,))
-        project(2, (0, 1, 2))
+        project(2, range(JT))
         upper11 = sb([P, HALF, PACK], BF16, "upper11", "part1_1")
         upper_halves(wx_raw[1, 1], upper11[:], on_scalar)
-        [q_wx[0, 1]] = split((wx_raw[0, 1],), upper01[:], "01", "upper0")
-        xb1 = sb([P, J, PACK], BF16, "xb1", "part0_1")
-        cast(x_raw[1], xb1[:], on_vector)
-        q_x[1] = quantise(flat(xb1[:]), "q_x1", J)
-        [q_wx[1, 1]] = split((wx_raw[1, 1],), upper11[:], "11", "part0_1")
-        project(2, (3,))
+        last_pass(0, upper01, "hi_lo0")
+        last_pass(1, upper11, None)
         project(3, range(JT))
         for pair in range(JT // 2):
             add_transposed()
-        base = [sb([P, J], F32, f"base{nt}") for nt in range(NT)]
-        for nt in range(NT):
+        base = {}
+        for nt in range(2):
+            base[nt] = sb([P, J], F32, f"base{nt}")
             nc.vector.tensor_tensor(base[nt][:], sums[nt][:], res_sb[:, nt, :], ALU.add)
+        for nt in range(2, NT):
+            moved = sb([P, J], F32, f"moved{nt}")
+            nc.scalar.copy(moved[:], sums[nt][:])
+            base[nt] = sb([P, J], F32, f"base{nt}", "hi_lo11" if nt == 2 else None)
+            nc.gpsimd.tensor_tensor(base[nt][:], moved[:], res_sb[:, nt, :], ALU.add)
+        skip = [bank(nt, f"skip{nt}") for nt in range(NT)]
+        for nt, a in ((0, 0), (1, 0), (2, 0), (3, 0), (0, 1), (1, 1), (2, 1), (3, 1)):
+            skip_pass(skip[nt], nt, a)
         for nt in range(NT):
-            skip = bank(nt, f"skip{nt}")
-            for a in range(PASSES):
-                skip_pass(skip, nt, a)
             done = sb([P, J], F32, f"done{nt}")
-            nc.vector.tensor_tensor(done[:], skip[:], base[nt][:], ALU.add)
+            nc.vector.tensor_tensor(done[:], skip[nt][:], base[nt][:], ALU.add)
             nc.sync.dma_start(out[nt * P : (nt + 1) * P, :], done[:])

@@ -22,7 +22,7 @@ PACK = 4
 PASSES = L // (P * PACK)
 JT = J // P
 NT = N // P
-RUN = 4
+RUN = 2
 HI_MASK = 0xFFF0FFF0 - (1 << 32)
 
 

@@ -57,8 +57,8 @@ def tile_list_interp_hl_res_kernel(
         w_w = sb([P, 2 * N], U8, "w_w")
         w_s = sb([P, N], U8, "w_s")
         ident = sb([P, P], F32, "ident")
-        iw_rows = [sb([P, P], F32, f"iw_rows{h}") for h in range(2)]
-        iw_cols = [sb([P, 2 * JT], F32, f"iw_cols{h}") for h in range(2)]
+        iw_rows = sb([P, P], F32, "iw_rows")
+        iw_cols = sb([P, G * JT], F32, "iw_cols")
 
         def bank(b, name):
             return psum.tile([P, N], F32, name=name, tag=f"bank{b}")
@@ -104,15 +104,14 @@ def tile_list_interp_hl_res_kernel(
             copy(words_view(dst), rows_view(raw))
 
         def load_weight(g):
-            rows = iw_rows[g // 2][(g % 2) * JT : (g % 2 + 1) * JT, :]
+            rows = iw_rows[g * JT : (g + 1) * JT, :]
             nc.sync.dma_start(rows, (iw0, iw1, iw2, iw3)[g].rearrange("(jt p) -> jt p", p=P))
 
         wx_raw, wx_whole, x_raw, q_wx, q_x = {}, {}, {}, {}, {}
-        nc.gpsimd.memset(iw_rows[0][:], 0.0)
+        nc.gpsimd.memset(iw_rows[:], 0.0)
         nc.gpsimd.memset(tab_s[:].bitcast(I32)[:, 0 : T // 8], 0)
         nc.vector.memset(tab_s[:].bitcast(I32)[:, T // 8 : T // 4], 0)
         nc.vector.memset(w_s[:].bitcast(I32), 0)
-        nc.vector.memset(iw_rows[1][:], 0.0)
         make_identity(nc, ident[:])
         nc.sync.dma_start(offsets[:], offs)
         nc.sync.dma_start(w_w[:].bitcast(I32), w_words[0].bitcast(I32))
@@ -134,20 +133,18 @@ def tile_list_interp_hl_res_kernel(
             wx_raw[0, a], wx_raw[1, a] = whole[:, :, 0:HALF], whole[:, :, HALF:N]
 
         load_table()
-        load_weight(1)
-        load_wx(0)
+        for g in range(1, G):
+            load_weight(g)
         load_scale_rows(w_s, w_scales)
-        load_weight(2)
-        load_weight(3)
+        load_wx(0)
         x_raw[0] = load_piece(x, 0, 0, J, "x0")
         load_wx(1)
         x_raw[1] = load_piece(x, 1, 0, J, "x1")
         load_res()
 
-        def turn_weights(h, b):
-            iw_ps = bank(b, f"iw_ps{h}")
-            nc.tensor.transpose(iw_ps[:, 0:P], iw_rows[h][:], ident[:])
-            nc.scalar.activation(iw_cols[h][:], iw_ps[:, 0 : 2 * JT], COPY)
+        iw_ps = bank(3, "iw_ps")
+        nc.tensor.transpose(iw_ps[:, 0:P], iw_rows[:], ident[:])
+        nc.scalar.activation(iw_cols[:], iw_ps[:, 0 : G * JT], COPY)
 
         sums = [psum.tile([P, J], F32, name=f"sum{nt}") for nt in range(NT)]
         got_s = sb([P, G * J], U8, "got_s")
@@ -180,8 +177,8 @@ def tile_list_interp_hl_res_kernel(
                     rhs=w_w[:].bitcast(FP4X4), rhs_scale=w_s[:], start=True, stop=True,
                 )
                 part = sb([P, N], F32, f"part{g}_{jt}")
-                col = (g % 2) * JT + jt
-                nc.scalar.activation(part[:], acc[:], COPY, scale=iw_cols[g // 2][:, col : col + 1])
+                col = g * JT + jt
+                nc.scalar.activation(part[:], acc[:], COPY, scale=iw_cols[:, col : col + 1])
                 waiting.append((g, jt, part))
                 if len(waiting) == JT + 2:
                     add_transposed()
@@ -197,16 +194,14 @@ def tile_list_interp_hl_res_kernel(
 
         on_vector, on_scalar = nc.vector.tensor_copy, nc.scalar.copy
         nc.vector.tensor_copy(got_s[:], tab_s[:].indirect(offsets[:]))
-        turn_weights(0, 0)
         gather_words(0, "tab_s")
         for g in range(1, G - 1):
             gather_words(g)
         upper0 = sb([P, N, PACK], BF16, "upper0")
-        upper_halves(wx_whole[0], upper0[:], on_scalar)
+        upper_halves(wx_whole[0], upper0[:], on_vector)
+        gather_words(G - 1)
         project(0, range(JT))
-        turn_weights(1, 0)
         both0 = truncate(upper0[:], N, "0")
-        gather_words(G - 1, "upper0")
         subtract(wx_raw[0, 0], both0, N, 0)
         xb0 = sb([P, J, PACK], BF16, "xb0")
         cast(x_raw[0], xb0[:], on_vector)
@@ -214,25 +209,23 @@ def tile_list_interp_hl_res_kernel(
         q_x[0] = quantise(flat(xb0[:]), "q_x0", J, "wx0")
         q_wx[0, 0], q_wx[1, 0] = quantise_split(both0, N, "0", "x0")
         project(1, range(JT))
-        q_x[1] = sb([P, J], U32, "q_x1_c"), sb([P, J], U8, "q_x1_s")
-
-        def last_pass(h, upper, tag):
-            cols = slice(h * HALF, (h + 1) * HALF)
-            both = truncate(upper[:], HALF, f"{h}1", tag)
-            xb = sb([P, HALF, PACK], BF16, f"xb1{h}", f"part{h}_1")
-            cast(x_raw[1][:, :, cols], xb[:], on_vector)
-            subtract(wx_raw[h, 1], both, HALF, 0)
-            nc.vector.quantize_mx(out=q_x[1][0][:, cols].bitcast(FP8X4), scales=q_x[1][1][:, cols], in_=flat(xb[:]))
-            [q_wx[h, 1]] = quantise_split(both, HALF, f"{h}1")
-
-        upper01 = sb([P, HALF, PACK], BF16, "upper01", "part0_1")
+        project(2, (0, 1))
+        upper01 = sb([P, HALF, PACK], BF16, "upper01", "part1_0")
         upper_halves(wx_raw[0, 1], upper01[:], on_scalar)
-        project(2, range(JT))
-        upper11 = sb([P, HALF, PACK], BF16, "upper11", "part1_1")
+        project(2, (2, 3))
+        project(3, (0, 1))
+        upper11 = sb([P, HALF, PACK], BF16, "upper11", "part2_0")
         upper_halves(wx_raw[1, 1], upper11[:], on_scalar)
-        last_pass(0, upper01, "hi_lo0")
-        last_pass(1, upper11, None)
-        project(3, range(JT))
+        project(3, (2, 3))
+        xb1 = sb([P, J, PACK], BF16, "xb1", "part2_2")
+        cast(x_raw[1], xb1[:], on_scalar)
+        both01 = truncate(upper01[:], HALF, "01", "hi_lo0")
+        subtract(wx_raw[0, 1], both01, HALF, 0)
+        both11 = truncate(upper11[:], HALF, "11")
+        [q_wx[0, 1]] = quantise_split(both01, HALF, "01")
+        subtract(wx_raw[1, 1], both11, HALF, 0)
+        q_x[1] = quantise(flat(xb1[:]), "q_x1", J)
+        [q_wx[1, 1]] = quantise_split(both11, HALF, "11")
         for pair in range(JT // 2):
             add_transposed()
         base = {}

@@ -22,7 +22,12 @@ PACK = 4
 PASSES = L // (P * PACK)
 JT = J // P
 NT = N // P
+HALF = N // 2
+QUAD = 32
+SPREAD = 8
+LIST_ROWS = 16
 RUN = 2
+PAIR = 2
 HI_MASK = 0xFFF0FFF0 - (1 << 32)
 
 
@@ -30,7 +35,6 @@ def tile_list_interp_hl_res_kernel(
     tc, tab_words, tab_scales, w_words, w_scales, x, wx, iw0, iw1, iw2, iw3, res, offs, out
 ):
     nc = tc.nc
-    HALF = N // 2
 
     def rows_view(ap):
         return ap.rearrange("p t (c i) -> p c t i", i=RUN)
@@ -38,134 +42,134 @@ def tile_list_interp_hl_res_kernel(
     def words_view(ap):
         return ap.rearrange("p (c i) t -> p c t i", i=RUN)
 
-    def load_scale_rows(plane, scales):
-        words = plane[:].bitcast(I32)
-        rows = scales[0].bitcast(I32).rearrange("(q r) c -> r q c", r=4)
-        for r in range(4):
-            nc.sync.dma_start(words[r:P:32, :], rows[r])
+    def flat(ap):
+        return ap.rearrange("p c t -> p (c t)")
+
+    def as_int32(tile):
+        return tile[:].bitcast(I32)
 
     with ExitStack() as ctx:
         held = ctx.enter_context(tc.tile_pool(name="held", bufs=1))
         psum = ctx.enter_context(tc.psum_pool(name="psum", bufs=1))
 
-        def sb(shape, dtype, name, tag=None):
-            return held.tile(shape, dtype, name=name, tag=tag or name, align_bytes=64)
-
-        offsets = held.tile([P, G * J // 16], U16, name="offsets")
-        tab_s = sb([P, T], U8, "tab_s")
-        tab_w = sb([P, T], U32, "tab_w")
-        w_w = sb([P, 2 * N], U8, "w_w")
-        w_s = sb([P, N], U8, "w_s")
-        ident = sb([P, P], F32, "ident")
-        iw_rows = sb([P, P], F32, "iw_rows")
-        iw_cols = sb([P, G * JT], F32, "iw_cols")
+        def sbuf(shape, dtype, name, after=None):
+            return held.tile(shape, dtype, name=name, tag=after or name, align_bytes=64)
 
         def bank(b, name):
             return psum.tile([P, N], F32, name=name, tag=f"bank{b}")
 
-        def load_piece(src, a, c0, width, name):
-            raw = sb([P, PACK * width], F32, name)[:].rearrange("p (t c) -> p t c", t=PACK)
-            rows = src[a * P * PACK : (a + 1) * P * PACK, c0 : c0 + width]
+        offsets = held.tile([P, G * J // LIST_ROWS], U16, name="offsets")
+        tab_s = sbuf([P, T], U8, "tab_s")
+        tab_w = sbuf([P, T], U32, "tab_w")
+        w_w = sbuf([P, 2 * N], U8, "w_w")
+        w_s = sbuf([P, N], U8, "w_s")
+        ident = sbuf([P, P], F32, "ident")
+        iw_rows = sbuf([P, P], F32, "iw_rows")
+        iw_cols = sbuf([P, G * JT], F32, "iw_cols")
+        got_s = sbuf([P, G * J], U8, "got_s")
+
+        def load_weights(g, queue):
+            rows = iw_rows[g * JT : (g + 1) * JT, :]
+            queue.dma_start(rows, (iw0, iw1, iw2, iw3)[g].rearrange("(jt p) -> jt p", p=P))
+
+        def load_pass(src, a, name):
+            raw = sbuf([P, PACK * N], F32, name)[:].rearrange("p (t c) -> p t c", t=PACK)
+            rows = src[a * P * PACK : (a + 1) * P * PACK, :]
             nc.sync.dma_start(raw, rows.rearrange("(p t) c -> p t c", t=PACK))
             return raw
 
-        def quantise(src, name, width, tag=None):
-            codes = sb([P, width], U32, name + "_c", tag)
-            scales = sb([P, width], U8, name + "_s")
-            nc.vector.quantize_mx(out=codes[:].bitcast(FP8X4), scales=scales[:], in_=src)
-            return codes, scales
+        nc.gpsimd.memset(as_int32(tab_s)[:, 0 : T // 8], 0)
+        nc.gpsimd.memset(iw_rows[:], 0.0)
+        load_weights(0, nc.gpsimd)
+        nc.vector.memset(as_int32(w_s), 0)
+        nc.vector.memset(as_int32(tab_s)[:, T // 8 : T // 4], 0)
+        nc.vector.memset(as_int32(got_s), 0)
+        make_identity(nc, ident[:])
+        nc.sync.dma_start(offsets[:], offs)
+        nc.sync.dma_start(as_int32(w_w), w_words[0].bitcast(I32))
+        w_rows = w_scales[0].bitcast(I32).rearrange("(q r) c -> r q c", r=4)
+        for r in range(4):
+            nc.sync.dma_start(as_int32(w_s)[r:P:QUAD, :], w_rows[r])
+        nc.sync.dma_start(as_int32(tab_s)[0:P:SPREAD, :], tab_scales[0].bitcast(I32))
+        nc.sync.dma_start(as_int32(tab_w), tab_words[0].rearrange("p t i -> p (t i)").bitcast(I32))
+        for g in range(1, G):
+            load_weights(g, nc.sync)
 
-        def flat(ap):
-            return ap.rearrange("p c t -> p (c t)")
+        iw_turned = bank(JT - 1, "iw_turned")
+        nc.tensor.transpose(iw_turned[:, 0:P], iw_rows[:], ident[:])
+        nc.scalar.activation(iw_cols[:], iw_turned[:, 0 : G * JT], COPY)
 
-        def upper_halves(raw, dst, copy):
+        sums = [psum.tile([P, J], F32, name=f"sum{nt}") for nt in range(NT)]
+
+        for h in range(2):
+            picked = sbuf([P, 2 * J], U8, f"picked{h}")
+            entries = offsets[:, 2 * h * J // LIST_ROWS : 2 * (h + 1) * J // LIST_ROWS]
+            nc.vector.tensor_copy(picked[:], tab_s[:].indirect(entries))
+            plane = as_int32(got_s)[:, h * J // 2 : (h + 1) * J // 2]
+            for r in range(4):
+                nc.sync.dma_start(plane[r:P:QUAD, :], as_int32(picked)[SPREAD * r : P : QUAD, :])
+
+        wx_raw, x_raw = {}, {}
+        for a in range(PASSES):
+            wx_raw[a] = load_pass(wx, a, f"wx{a}")
+            x_raw[a] = load_pass(x, a, f"x{a}")
+        res_sb = sbuf([P, NT, J], F32, "res_sb")
+        nc.sync.dma_start(res_sb[:], res.rearrange("(nt p) j -> p nt j", p=P))
+
+        got_w, q_wx, q_x = {}, {}, {}
+
+        def gather_words(g):
+            got_w[g] = sbuf([P, J], U32, f"got_w{g}")
+            entries = offsets[:, g * J // LIST_ROWS : (g + 1) * J // LIST_ROWS]
+            nc.vector.tensor_copy(got_w[g][:], tab_w[:].indirect(entries))
+
+        def half(raw, h):
+            return raw[:, :, h * HALF : (h + 1) * HALF]
+
+        def upper_halves(raw, name, copy, after=None):
+            upper = sbuf([P, raw.shape[2], PACK], BF16, name, after)
             tops = raw.bitcast(BF16).rearrange("p t (c two) -> p t c two", two=2)[:, :, :, 1]
-            copy(words_view(dst), rows_view(tops))
+            copy(words_view(upper[:]), rows_view(tops))
+            return upper
 
-        def truncate(upper, width, name, tag=None):
-            both = sb([P, 2 * width, PACK], BF16, "hi_lo" + name, tag)
+        def truncate(upper, width, name, after=None):
+            both = sbuf([P, 2 * width, PACK], BF16, name, after)
             nc.vector.tensor_scalar(
-                flat(both[:, 0:width, :]).bitcast(I32), flat(upper).bitcast(I32), HI_MASK, None, ALU.bitwise_and
+                flat(both[:, 0:width, :]).bitcast(I32), flat(upper[:]).bitcast(I32), HI_MASK, None, ALU.bitwise_and
             )
             return both
 
-        def subtract(raw, both, width, i):
-            hi = both[:, i * HALF : (i + 1) * HALF, :]
-            lo = both[:, width + i * HALF : width + (i + 1) * HALF, :]
+        def subtract(raw, both, width, first):
+            hi = both[:, first : first + HALF, :]
+            lo = both[:, width + first : width + first + HALF, :]
             nc.vector.tensor_tensor(words_view(lo), rows_view(raw), words_view(hi), ALU.subtract)
 
-        def quantise_split(both, width, name, tag=None):
-            codes, scales = quantise(flat(both[:]), "q" + name, 2 * width, tag)
-            return [
-                [(codes, scales, part * width + i * HALF) for part in range(2)] for i in range(width // HALF)
-            ]
+        def cast(raw, name, copy, after=None):
+            rounded = sbuf([P, J, PACK], BF16, name, after)
+            copy(words_view(rounded[:]), rows_view(raw))
+            return rounded
 
-        def cast(raw, dst, copy):
-            copy(words_view(dst), rows_view(raw))
+        def quantise(src, name, width, after=None):
+            codes = sbuf([P, width], U32, name + "_codes", after)
+            scales = sbuf([P, width], U8, name + "_scales")
+            nc.vector.quantize_mx(out=codes[:].bitcast(FP8X4), scales=scales[:], in_=flat(src[:]))
+            return codes, scales
 
-        def load_weight(g):
-            rows = iw_rows[g * JT : (g + 1) * JT, :]
-            nc.sync.dma_start(rows, (iw0, iw1, iw2, iw3)[g].rearrange("(jt p) -> jt p", p=P))
-
-        wx_raw, wx_whole, x_raw, q_wx, q_x = {}, {}, {}, {}, {}
-        nc.gpsimd.memset(iw_rows[:], 0.0)
-        nc.gpsimd.memset(tab_s[:].bitcast(I32)[:, 0 : T // 8], 0)
-        nc.vector.memset(tab_s[:].bitcast(I32)[:, T // 8 : T // 4], 0)
-        nc.vector.memset(w_s[:].bitcast(I32), 0)
-        make_identity(nc, ident[:])
-        nc.sync.dma_start(offsets[:], offs)
-        nc.sync.dma_start(w_w[:].bitcast(I32), w_words[0].bitcast(I32))
-        load_weight(0)
-        load_scale_rows(tab_s, tab_scales)
-        res_sb = sb([P, NT, J], F32, "res_sb")
-
-        def load_table():
-            nc.sync.dma_start(
-                tab_w[:].bitcast(I32), tab_words[0].rearrange("p t i -> p (t i)").bitcast(I32)
-            )
-
-        def load_res():
-            nc.sync.dma_start(res_sb[:], res.rearrange("(nt p) j -> p nt j", p=P))
-
-        def load_wx(a):
-            whole = load_piece(wx, a, 0, N, f"wx{a}")
-            wx_whole[a] = whole
-            wx_raw[0, a], wx_raw[1, a] = whole[:, :, 0:HALF], whole[:, :, HALF:N]
-
-        load_table()
-        for g in range(1, G):
-            load_weight(g)
-        load_scale_rows(w_s, w_scales)
-        load_wx(0)
-        x_raw[0] = load_piece(x, 0, 0, J, "x0")
-        load_wx(1)
-        x_raw[1] = load_piece(x, 1, 0, J, "x1")
-        load_res()
-
-        iw_ps = bank(3, "iw_ps")
-        nc.tensor.transpose(iw_ps[:, 0:P], iw_rows[:], ident[:])
-        nc.scalar.activation(iw_cols[:], iw_ps[:, 0 : G * JT], COPY)
-
-        sums = [psum.tile([P, J], F32, name=f"sum{nt}") for nt in range(NT)]
-        got_s = sb([P, G * J], U8, "got_s")
-        got_w = {}
-
-        def gather_words(g, tag=None):
-            got_w[g] = sb([P, J], U32, f"got_w{g}", tag)
-            picks = offsets[:, g * J // 16 : (g + 1) * J // 16]
-            nc.vector.tensor_copy(got_w[g][:], tab_w[:].indirect(picks))
+        def quantise_split(both, width, name, after=None):
+            codes, scales = quantise(both, name, 2 * width, after)
+            return [[(codes, scales, part * width + first) for part in range(2)] for first in range(0, width, HALF)]
 
         waiting = []
 
         def add_transposed():
-            pair = waiting[0:2]
+            pair = waiting[0:PAIR]
             for item in pair:
                 waiting.remove(item)
             for g, jt, part in reversed(pair):
                 for nt in range(NT):
                     nc.tensor.matmul(
                         sums[nt][:, jt * P : (jt + 1) * P], part[:, nt * P : (nt + 1) * P], ident[:],
-                        start=(g, jt) == (0, 1), stop=(g, jt) == (G - 1, JT - 2), is_transpose=True,
+                        start=(g, jt) == (0, PAIR - 1), stop=(g, jt) == (G - 1, JT - PAIR), is_transpose=True,
                     )
 
         def project(g, tiles):
@@ -176,11 +180,11 @@ def tile_list_interp_hl_res_kernel(
                     lhsT_scale=got_s[:, g * J + jt * P : g * J + (jt + 1) * P],
                     rhs=w_w[:].bitcast(FP4X4), rhs_scale=w_s[:], start=True, stop=True,
                 )
-                part = sb([P, N], F32, f"part{g}_{jt}")
+                part = sbuf([P, N], F32, f"part{g}_{jt}")
                 col = g * JT + jt
                 nc.scalar.activation(part[:], acc[:], COPY, scale=iw_cols[:, col : col + 1])
                 waiting.append((g, jt, part))
-                if len(waiting) == JT + 2:
+                if len(waiting) == JT + PAIR:
                     add_transposed()
 
         def skip_pass(acc, nt, a):
@@ -193,54 +197,56 @@ def tile_list_interp_hl_res_kernel(
                 )
 
         on_vector, on_scalar = nc.vector.tensor_copy, nc.scalar.copy
-        nc.vector.tensor_copy(got_s[:], tab_s[:].indirect(offsets[:]))
-        gather_words(0, "tab_s")
-        for g in range(1, G - 1):
+        first_tiles, last_tiles = range(0, PAIR), range(PAIR, JT)
+
+        for g in range(G - 1):
             gather_words(g)
-        upper0 = sb([P, N, PACK], BF16, "upper0")
-        upper_halves(wx_whole[0], upper0[:], on_vector)
+        upper0 = upper_halves(wx_raw[0], "upper0", on_vector)
         gather_words(G - 1)
         project(0, range(JT))
-        both0 = truncate(upper0[:], N, "0")
-        subtract(wx_raw[0, 0], both0, N, 0)
-        xb0 = sb([P, J, PACK], BF16, "xb0")
-        cast(x_raw[0], xb0[:], on_vector)
-        subtract(wx_raw[1, 0], both0, N, 1)
-        q_x[0] = quantise(flat(xb0[:]), "q_x0", J, "wx0")
-        q_wx[0, 0], q_wx[1, 0] = quantise_split(both0, N, "0", "x0")
+        both0 = truncate(upper0, N, "both0")
+        subtract(half(wx_raw[0], 0), both0, N, 0)
+        rounded0 = cast(x_raw[0], "rounded0", on_vector)
+        subtract(half(wx_raw[0], 1), both0, N, HALF)
+        q_x[0] = quantise(rounded0, "q_x0", J, after="wx0")
+        q_wx[0, 0], q_wx[1, 0] = quantise_split(both0, N, "q_wx0", after="x0")
+
         project(1, range(JT))
-        project(2, (0, 1))
-        upper01 = sb([P, HALF, PACK], BF16, "upper01", "part1_0")
-        upper_halves(wx_raw[0, 1], upper01[:], on_scalar)
-        project(2, (2, 3))
-        project(3, (0, 1))
-        upper11 = sb([P, HALF, PACK], BF16, "upper11", "part2_0")
-        upper_halves(wx_raw[1, 1], upper11[:], on_scalar)
-        project(3, (2, 3))
-        xb1 = sb([P, J, PACK], BF16, "xb1", "part2_2")
-        cast(x_raw[1], xb1[:], on_scalar)
-        both01 = truncate(upper01[:], HALF, "01", "hi_lo0")
-        subtract(wx_raw[0, 1], both01, HALF, 0)
-        both11 = truncate(upper11[:], HALF, "11")
-        [q_wx[0, 1]] = quantise_split(both01, HALF, "01")
-        subtract(wx_raw[1, 1], both11, HALF, 0)
-        q_x[1] = quantise(flat(xb1[:]), "q_x1", J)
-        [q_wx[1, 1]] = quantise_split(both11, HALF, "11")
-        for pair in range(JT // 2):
+        project(2, first_tiles)
+        upper01 = upper_halves(half(wx_raw[1], 0), "upper01", on_scalar, after="part1_0")
+        project(2, last_tiles)
+        project(3, first_tiles)
+        upper11 = upper_halves(half(wx_raw[1], 1), "upper11", on_scalar, after="part2_0")
+        project(3, last_tiles)
+        rounded1 = cast(x_raw[1], "rounded1", on_scalar, after="part2_2")
+
+        both01 = truncate(upper01, HALF, "both01", after="both0")
+        subtract(half(wx_raw[1], 0), both01, HALF, 0)
+        both11 = truncate(upper11, HALF, "both11")
+        [q_wx[0, 1]] = quantise_split(both01, HALF, "q_wx01")
+        subtract(half(wx_raw[1], 1), both11, HALF, 0)
+        q_x[1] = quantise(rounded1, "q_x1", J)
+        [q_wx[1, 1]] = quantise_split(both11, HALF, "q_wx11")
+        for pair in range(JT // PAIR):
             add_transposed()
+
         base = {}
-        for nt in range(2):
-            base[nt] = sb([P, J], F32, f"base{nt}")
+        for nt in range(NT // 2):
+            base[nt] = sbuf([P, J], F32, f"base{nt}")
             nc.vector.tensor_tensor(base[nt][:], sums[nt][:], res_sb[:, nt, :], ALU.add)
-        for nt in range(2, NT):
-            moved = sb([P, J], F32, f"moved{nt}")
+        behind = "both11"
+        for nt in range(NT // 2, NT):
+            moved = sbuf([P, J], F32, f"moved{nt}")
             nc.scalar.copy(moved[:], sums[nt][:])
-            base[nt] = sb([P, J], F32, f"base{nt}", "hi_lo11" if nt == 2 else None)
+            base[nt] = sbuf([P, J], F32, f"base{nt}", after=behind)
             nc.gpsimd.tensor_tensor(base[nt][:], moved[:], res_sb[:, nt, :], ALU.add)
+            behind = f"moved{nt}"
+
         skip = [bank(nt, f"skip{nt}") for nt in range(NT)]
-        for nt, a in ((0, 0), (1, 0), (2, 0), (3, 0), (0, 1), (1, 1), (2, 1), (3, 1)):
-            skip_pass(skip[nt], nt, a)
+        for a in range(PASSES):
+            for nt in range(NT):
+                skip_pass(skip[nt], nt, a)
         for nt in range(NT):
-            done = sb([P, J], F32, f"done{nt}")
+            done = sbuf([P, J], F32, f"done{nt}")
             nc.vector.tensor_tensor(done[:], skip[nt][:], base[nt][:], ALU.add)
             nc.sync.dma_start(out[nt * P : (nt + 1) * P, :], done[:])

@@ -27,7 +27,7 @@ QUAD = 32
 SPREAD = 8
 LIST_ROWS = 16
 RUN = 2
-PAIR = 2
+RUN_PARTS = 3
 HI_MASK = 0xFFF0FFF0 - (1 << 32)
 
 
@@ -64,12 +64,12 @@ def tile_list_interp_hl_res_kernel(
         w_w = sbuf([P, 2 * N], U8, "w_w")
         w_s = sbuf([P, N], U8, "w_s")
         ident = sbuf([P, P], F32, "ident")
-        iw_rows = sbuf([P, P], F32, "iw_rows")
-        iw_cols = sbuf([P, G * JT], F32, "iw_cols")
+        iw_rows = [sbuf([P, P], F32, f"iw_rows{h}") for h in range(2)]
+        iw_cols = [sbuf([P, 2 * JT], F32, f"iw_cols{h}") for h in range(2)]
         got_s = sbuf([P, G * J], U8, "got_s")
 
         def load_weights(g, queue):
-            rows = iw_rows[g * JT : (g + 1) * JT, :]
+            rows = iw_rows[g // 2][g % 2 * JT : (g % 2 + 1) * JT, :]
             queue.dma_start(rows, (iw0, iw1, iw2, iw3)[g].rearrange("(jt p) -> jt p", p=P))
 
         def load_pass(src, a, name):
@@ -79,28 +79,34 @@ def tile_list_interp_hl_res_kernel(
             return raw
 
         nc.gpsimd.memset(as_int32(tab_s)[:, 0 : T // 8], 0)
-        nc.gpsimd.memset(iw_rows[:], 0.0)
-        load_weights(0, nc.gpsimd)
+        for h in range(2):
+            nc.gpsimd.memset(iw_rows[h][:], 0.0)
+        make_identity(nc, ident[:])
+        for g in range(2, G):
+            load_weights(g, nc.gpsimd)
         nc.vector.memset(as_int32(w_s), 0)
         nc.vector.memset(as_int32(tab_s)[:, T // 8 : T // 4], 0)
         nc.vector.memset(as_int32(got_s), 0)
-        make_identity(nc, ident[:])
         nc.sync.dma_start(offsets[:], offs)
         nc.sync.dma_start(as_int32(w_w), w_words[0].bitcast(I32))
+        nc.sync.dma_start(as_int32(tab_s)[0:P:SPREAD, :], tab_scales[0].bitcast(I32))
         w_rows = w_scales[0].bitcast(I32).rearrange("(q r) c -> r q c", r=4)
         for r in range(4):
-            nc.sync.dma_start(as_int32(w_s)[r:P:QUAD, :], w_rows[r])
-        nc.sync.dma_start(as_int32(tab_s)[0:P:SPREAD, :], tab_scales[0].bitcast(I32))
+            nc.scalar.dma_start(as_int32(w_s)[r:P:QUAD, :], w_rows[r])
         nc.sync.dma_start(as_int32(tab_w), tab_words[0].rearrange("p t i -> p (t i)").bitcast(I32))
-        for g in range(1, G):
+        for g in range(2):
             load_weights(g, nc.sync)
 
-        iw_turned = bank(JT - 1, "iw_turned")
-        nc.tensor.transpose(iw_turned[:, 0:P], iw_rows[:], ident[:])
-        nc.scalar.activation(iw_cols[:], iw_turned[:, 0 : G * JT], COPY)
+        def turn_weights(h, b):
+            iw_turned = bank(b, f"iw_turned{h}")
+            nc.tensor.transpose(iw_turned[:, 0:P], iw_rows[h][:], ident[:])
+            nc.scalar.activation(iw_cols[h][:], iw_turned[:, 0 : 2 * JT], COPY)
+
+        turn_weights(0, JT - 1)
 
         sums = [psum.tile([P, J], F32, name=f"sum{nt}") for nt in range(NT)]
 
+        wx_raw, x_raw = {}, {}
         for h in range(2):
             picked = sbuf([P, 2 * J], U8, f"picked{h}")
             entries = offsets[:, 2 * h * J // LIST_ROWS : 2 * (h + 1) * J // LIST_ROWS]
@@ -108,11 +114,12 @@ def tile_list_interp_hl_res_kernel(
             plane = as_int32(got_s)[:, h * J // 2 : (h + 1) * J // 2]
             for r in range(4):
                 nc.sync.dma_start(plane[r:P:QUAD, :], as_int32(picked)[SPREAD * r : P : QUAD, :])
+            if h == 0:
+                wx_raw[0] = load_pass(wx, 0, "wx0")
 
-        wx_raw, x_raw = {}, {}
-        for a in range(PASSES):
-            wx_raw[a] = load_pass(wx, a, f"wx{a}")
-            x_raw[a] = load_pass(x, a, f"x{a}")
+        wx_raw[1] = load_pass(wx, 1, "wx1")
+        x_raw[0] = load_pass(x, 0, "x0")
+        x_raw[1] = load_pass(x, 1, "x1")
         res_sb = sbuf([P, NT, J], F32, "res_sb")
         nc.sync.dma_start(res_sb[:], res.rearrange("(nt p) j -> p nt j", p=P))
 
@@ -135,7 +142,7 @@ def tile_list_interp_hl_res_kernel(
         def truncate(upper, width, name, after=None):
             both = sbuf([P, 2 * width, PACK], BF16, name, after)
             nc.vector.tensor_scalar(
-                flat(both[:, 0:width, :]).bitcast(I32), flat(upper[:]).bitcast(I32), HI_MASK, None, ALU.bitwise_and
+                flat(both[:, 0:width, :]).bitcast(I32), flat(upper).bitcast(I32), HI_MASK, None, ALU.bitwise_and
             )
             return both
 
@@ -161,15 +168,14 @@ def tile_list_interp_hl_res_kernel(
 
         waiting = []
 
-        def add_transposed():
-            pair = waiting[0:PAIR]
-            for item in pair:
+        def add_transposed(items):
+            for item in items:
                 waiting.remove(item)
-            for g, jt, part in reversed(pair):
+                g, jt, part = item
                 for nt in range(NT):
                     nc.tensor.matmul(
                         sums[nt][:, jt * P : (jt + 1) * P], part[:, nt * P : (nt + 1) * P], ident[:],
-                        start=(g, jt) == (0, PAIR - 1), stop=(g, jt) == (G - 1, JT - PAIR), is_transpose=True,
+                        start=(g, jt) == (0, JT - 1), stop=(g, jt) == (G - 1, JT - 1), is_transpose=True,
                     )
 
         def project(g, tiles):
@@ -181,11 +187,13 @@ def tile_list_interp_hl_res_kernel(
                     rhs=w_w[:].bitcast(FP4X4), rhs_scale=w_s[:], start=True, stop=True,
                 )
                 part = sbuf([P, N], F32, f"part{g}_{jt}")
-                col = g * JT + jt
-                nc.scalar.activation(part[:], acc[:], COPY, scale=iw_cols[:, col : col + 1])
+                col = g % 2 * JT + jt
+                nc.scalar.activation(part[:], acc[:], COPY, scale=iw_cols[g // 2][:, col : col + 1])
                 waiting.append((g, jt, part))
-                if len(waiting) == JT + PAIR:
-                    add_transposed()
+            if g > 0:
+                newest = waiting[-JT - 1]
+                older = waiting[0 : RUN_PARTS - 1] if g < G - 1 else [w for w in waiting if w is not newest]
+                add_transposed([newest] + older)
 
         def skip_pass(acc, nt, a):
             for s, (codes, scales, first) in enumerate(q_wx[nt // 2, a]):
@@ -197,56 +205,49 @@ def tile_list_interp_hl_res_kernel(
                 )
 
         on_vector, on_scalar = nc.vector.tensor_copy, nc.scalar.copy
-        first_tiles, last_tiles = range(0, PAIR), range(PAIR, JT)
 
         for g in range(G - 1):
             gather_words(g)
         upper0 = upper_halves(wx_raw[0], "upper0", on_vector)
         gather_words(G - 1)
         project(0, range(JT))
-        both0 = truncate(upper0, N, "both0")
+        both0 = truncate(upper0[:], N, "both0")
         subtract(half(wx_raw[0], 0), both0, N, 0)
-        rounded0 = cast(x_raw[0], "rounded0", on_vector)
         subtract(half(wx_raw[0], 1), both0, N, HALF)
+        rounded0 = cast(x_raw[0], "rounded0", on_vector)
+        q_wx[0, 0], q_wx[1, 0] = quantise_split(both0, N, "q_wx0")
         q_x[0] = quantise(rounded0, "q_x0", J, after="wx0")
-        q_wx[0, 0], q_wx[1, 0] = quantise_split(both0, N, "q_wx0", after="x0")
 
-        project(1, range(JT))
-        project(2, first_tiles)
-        upper01 = upper_halves(half(wx_raw[1], 0), "upper01", on_scalar, after="part1_0")
-        project(2, last_tiles)
-        project(3, first_tiles)
-        upper11 = upper_halves(half(wx_raw[1], 1), "upper11", on_scalar, after="part2_0")
-        project(3, last_tiles)
-        rounded1 = cast(x_raw[1], "rounded1", on_scalar, after="part2_2")
+        turn_weights(1, 0)
+        for g in range(1, G - 1):
+            project(g, range(JT))
+        upper1 = upper_halves(wx_raw[1], "upper1", on_scalar, after="got_w2")
+        project(G - 1, range(JT))
+        rounded1 = cast(x_raw[1], "rounded1", on_scalar, after="got_w3")
 
-        both01 = truncate(upper01, HALF, "both01", after="both0")
+        both01 = truncate(upper1[:, 0:HALF, :], HALF, "both01", after="x0")
+        both11 = truncate(upper1[:, HALF:N, :], HALF, "both11", after="rounded0")
         subtract(half(wx_raw[1], 0), both01, HALF, 0)
-        both11 = truncate(upper11, HALF, "both11")
-        [q_wx[0, 1]] = quantise_split(both01, HALF, "q_wx01")
         subtract(half(wx_raw[1], 1), both11, HALF, 0)
-        q_x[1] = quantise(rounded1, "q_x1", J)
+        [q_wx[0, 1]] = quantise_split(both01, HALF, "q_wx01")
         [q_wx[1, 1]] = quantise_split(both11, HALF, "q_wx11")
-        for pair in range(JT // PAIR):
-            add_transposed()
+        q_x[1] = quantise(rounded1, "q_x1", J)
 
-        base = {}
+        late = sbuf([P, 2 * NT * J], F32, "late", after="got_w3")
+        base = [late[:, nt * J : (nt + 1) * J] for nt in range(NT)]
+        done = [late[:, (NT + nt) * J : (NT + nt + 1) * J] for nt in range(NT)]
         for nt in range(NT // 2):
-            base[nt] = sbuf([P, J], F32, f"base{nt}")
-            nc.vector.tensor_tensor(base[nt][:], sums[nt][:], res_sb[:, nt, :], ALU.add)
-        behind = "both11"
+            nc.vector.tensor_tensor(base[nt], sums[nt][:], res_sb[:, nt, :], ALU.add)
+        moved = sbuf([P, NT * J], F32, "moved", after="x1")
         for nt in range(NT // 2, NT):
-            moved = sbuf([P, J], F32, f"moved{nt}")
-            nc.scalar.copy(moved[:], sums[nt][:])
-            base[nt] = sbuf([P, J], F32, f"base{nt}", after=behind)
-            nc.gpsimd.tensor_tensor(base[nt][:], moved[:], res_sb[:, nt, :], ALU.add)
-            behind = f"moved{nt}"
+            cols = slice(nt * J, (nt + 1) * J)
+            nc.scalar.copy(moved[:, cols], sums[nt][:])
+            nc.gpsimd.tensor_tensor(base[nt], moved[:, cols], res_sb[:, nt, :], ALU.add)
 
         skip = [bank(nt, f"skip{nt}") for nt in range(NT)]
         for a in range(PASSES):
             for nt in range(NT):
                 skip_pass(skip[nt], nt, a)
         for nt in range(NT):
-            done = sbuf([P, J], F32, f"done{nt}")
-            nc.vector.tensor_tensor(done[:], skip[nt][:], base[nt][:], ALU.add)
-            nc.sync.dma_start(out[nt * P : (nt + 1) * P, :], done[:])
+            nc.vector.tensor_tensor(done[nt], skip[nt][:], base[nt], ALU.add)
+            nc.sync.dma_start(out[nt * P : (nt + 1) * P, :], done[nt])

@@ -27,7 +27,7 @@ QUAD = 32
 SPREAD = 8
 LIST_ROWS = 16
 RUN = 2
-RUN_PARTS = 3
+BLOCK = 8
 HI_MASK = 0xFFF0FFF0 - (1 << 32)
 
 
@@ -64,49 +64,52 @@ def tile_list_interp_hl_res_kernel(
         w_w = sbuf([P, 2 * N], U8, "w_w")
         w_s = sbuf([P, N], U8, "w_s")
         ident = sbuf([P, P], F32, "ident")
-        iw_rows = [sbuf([P, P], F32, f"iw_rows{h}") for h in range(2)]
-        iw_cols = [sbuf([P, 2 * JT], F32, f"iw_cols{h}") for h in range(2)]
+        iw_rows = sbuf([P, P], F32, "iw_rows")
+        iw_cols = sbuf([P, 2 * JT], F32, "iw_cols")
         got_s = sbuf([P, G * J], U8, "got_s")
+        weights = (iw0, iw1, iw2, iw3)
+        scale_of = {}
 
-        def load_weights(g, queue):
-            rows = iw_rows[g // 2][g % 2 * JT : (g % 2 + 1) * JT, :]
-            queue.dma_start(rows, (iw0, iw1, iw2, iw3)[g].rearrange("(jt p) -> jt p", p=P))
+        def load_rows(g):
+            nc.sync.dma_start(iw_rows[g * JT : (g + 1) * JT, :], weights[g].rearrange("(jt p) -> jt p", p=P))
+            for jt in range(JT):
+                scale_of[g, jt] = iw_cols[:, g * JT + jt : g * JT + jt + 1]
 
-        def load_pass(src, a, name):
-            raw = sbuf([P, PACK * N], F32, name)[:].rearrange("p (t c) -> p t c", t=PACK)
-            rows = src[a * P * PACK : (a + 1) * P * PACK, :]
+        def load_columns(g):
+            cols = sbuf([P, JT, BLOCK], F32, f"iw_cols{g}")
+            with nc.allow_non_contiguous_dma(reason="one weight a partition and tile"):
+                nc.sync.dma_start(cols[:, :, 0], weights[g].rearrange("(jt p) -> p jt", p=P))
+            for jt in range(JT):
+                scale_of[g, jt] = cols[:, jt, 0:1]
+
+        def load_pass(src, a, name, first=0, width=N):
+            raw = sbuf([P, PACK * width], F32, name)[:].rearrange("p (t c) -> p t c", t=PACK)
+            rows = src[a * P * PACK : (a + 1) * P * PACK, first : first + width]
             nc.sync.dma_start(raw, rows.rearrange("(p t) c -> p t c", t=PACK))
             return raw
 
         nc.gpsimd.memset(as_int32(tab_s)[:, 0 : T // 8], 0)
-        for h in range(2):
-            nc.gpsimd.memset(iw_rows[h][:], 0.0)
+        nc.gpsimd.memset(iw_rows[:], 0.0)
         make_identity(nc, ident[:])
-        for g in range(2, G):
-            load_weights(g, nc.gpsimd)
-        nc.vector.memset(as_int32(w_s), 0)
         nc.vector.memset(as_int32(tab_s)[:, T // 8 : T // 4], 0)
+        nc.vector.memset(as_int32(w_s), 0)
         nc.vector.memset(as_int32(got_s), 0)
         nc.sync.dma_start(offsets[:], offs)
         nc.sync.dma_start(as_int32(w_w), w_words[0].bitcast(I32))
         nc.sync.dma_start(as_int32(tab_s)[0:P:SPREAD, :], tab_scales[0].bitcast(I32))
         w_rows = w_scales[0].bitcast(I32).rearrange("(q r) c -> r q c", r=4)
         for r in range(4):
-            nc.scalar.dma_start(as_int32(w_s)[r:P:QUAD, :], w_rows[r])
+            nc.sync.dma_start(as_int32(w_s)[r:P:QUAD, :], w_rows[r])
         nc.sync.dma_start(as_int32(tab_w), tab_words[0].rearrange("p t i -> p (t i)").bitcast(I32))
         for g in range(2):
-            load_weights(g, nc.sync)
+            load_rows(g)
 
-        def turn_weights(h, b):
-            iw_turned = bank(b, f"iw_turned{h}")
-            nc.tensor.transpose(iw_turned[:, 0:P], iw_rows[h][:], ident[:])
-            nc.scalar.activation(iw_cols[h][:], iw_turned[:, 0 : 2 * JT], COPY)
-
-        turn_weights(0, JT - 1)
+        iw_turned = bank(JT - 1, "iw_turned")
+        nc.tensor.transpose(iw_turned[:, 0:P], iw_rows[:], ident[:])
+        nc.scalar.activation(iw_cols[:], iw_turned[:, 0 : 2 * JT], COPY)
 
         sums = [psum.tile([P, J], F32, name=f"sum{nt}") for nt in range(NT)]
 
-        wx_raw, x_raw = {}, {}
         for h in range(2):
             picked = sbuf([P, 2 * J], U8, f"picked{h}")
             entries = offsets[:, 2 * h * J // LIST_ROWS : 2 * (h + 1) * J // LIST_ROWS]
@@ -115,11 +118,13 @@ def tile_list_interp_hl_res_kernel(
             for r in range(4):
                 nc.sync.dma_start(plane[r:P:QUAD, :], as_int32(picked)[SPREAD * r : P : QUAD, :])
             if h == 0:
-                wx_raw[0] = load_pass(wx, 0, "wx0")
-
-        wx_raw[1] = load_pass(wx, 1, "wx1")
-        x_raw[0] = load_pass(x, 0, "x0")
-        x_raw[1] = load_pass(x, 1, "x1")
+                wx0 = load_pass(wx, 0, "wx0")
+        x0 = load_pass(x, 0, "x0")
+        wx1 = []
+        for h in range(2):
+            wx1.append(load_pass(wx, 1, f"wx1{h}", h * HALF, HALF))
+            load_columns(2 + h)
+        x1 = load_pass(x, 1, "x1")
         res_sb = sbuf([P, NT, J], F32, "res_sb")
         nc.sync.dma_start(res_sb[:], res.rearrange("(nt p) j -> p nt j", p=P))
 
@@ -133,22 +138,15 @@ def tile_list_interp_hl_res_kernel(
         def half(raw, h):
             return raw[:, :, h * HALF : (h + 1) * HALF]
 
-        def upper_halves(raw, name, copy, after=None):
-            upper = sbuf([P, raw.shape[2], PACK], BF16, name, after)
+        def upper_halves(raw, upper, copy):
             tops = raw.bitcast(BF16).rearrange("p t (c two) -> p t c two", two=2)[:, :, :, 1]
-            copy(words_view(upper[:]), rows_view(tops))
-            return upper
+            copy(words_view(upper), rows_view(tops))
 
-        def truncate(upper, width, name, after=None):
-            both = sbuf([P, 2 * width, PACK], BF16, name, after)
-            nc.vector.tensor_scalar(
-                flat(both[:, 0:width, :]).bitcast(I32), flat(upper).bitcast(I32), HI_MASK, None, ALU.bitwise_and
-            )
-            return both
+        def truncate(upper, hi):
+            nc.vector.tensor_scalar(hi.bitcast(I32), upper.bitcast(I32), HI_MASK, None, ALU.bitwise_and)
 
-        def subtract(raw, both, width, first):
-            hi = both[:, first : first + HALF, :]
-            lo = both[:, width + first : width + first + HALF, :]
+        def subtract(raw, both, h):
+            hi, lo = (both[:, h, s, :].rearrange("p (c t) -> p c t", t=PACK) for s in range(2))
             nc.vector.tensor_tensor(words_view(lo), rows_view(raw), words_view(hi), ALU.subtract)
 
         def cast(raw, name, copy, after=None):
@@ -156,48 +154,41 @@ def tile_list_interp_hl_res_kernel(
             copy(words_view(rounded[:]), rows_view(raw))
             return rounded
 
-        def quantise(src, name, width, after=None):
+        def quantise(src, name, after=None):
+            width = src.shape[1] // PACK
             codes = sbuf([P, width], U32, name + "_codes", after)
             scales = sbuf([P, width], U8, name + "_scales")
-            nc.vector.quantize_mx(out=codes[:].bitcast(FP8X4), scales=scales[:], in_=flat(src[:]))
+            nc.vector.quantize_mx(out=codes[:].bitcast(FP8X4), scales=scales[:], in_=src)
             return codes, scales
 
-        def quantise_split(both, width, name, after=None):
-            codes, scales = quantise(both, name, 2 * width, after)
-            return [[(codes, scales, part * width + first) for part in range(2)] for first in range(0, width, HALF)]
+        parts = {}
 
-        waiting = []
-
-        def add_transposed(items):
-            for item in items:
-                waiting.remove(item)
-                g, jt, part = item
+        def add_transposed(*tiles):
+            for g, jt in tiles:
                 for nt in range(NT):
                     nc.tensor.matmul(
-                        sums[nt][:, jt * P : (jt + 1) * P], part[:, nt * P : (nt + 1) * P], ident[:],
-                        start=(g, jt) == (0, JT - 1), stop=(g, jt) == (G - 1, JT - 1), is_transpose=True,
+                        sums[nt][:, jt * P : (jt + 1) * P], parts[g, jt][:, nt * P : (nt + 1) * P], ident[:],
+                        start=(g, jt) == (0, JT - 1), stop=(g, jt) == (G - 1, JT - 2), is_transpose=True,
                     )
 
-        def project(g, tiles):
-            for jt in tiles:
+        def project(g):
+            for jt in range(JT):
                 acc = bank(jt, f"acc{g}_{jt}")
                 nc.tensor.matmul_mx(
                     acc[:], lhsT=got_w[g][:, jt * P : (jt + 1) * P].bitcast(FP8X4),
                     lhsT_scale=got_s[:, g * J + jt * P : g * J + (jt + 1) * P],
                     rhs=w_w[:].bitcast(FP4X4), rhs_scale=w_s[:], start=True, stop=True,
                 )
-                part = sbuf([P, N], F32, f"part{g}_{jt}")
-                col = g % 2 * JT + jt
-                nc.scalar.activation(part[:], acc[:], COPY, scale=iw_cols[g // 2][:, col : col + 1])
-                waiting.append((g, jt, part))
+                parts[g, jt] = sbuf([P, N], F32, f"part{g}_{jt}")
+                nc.scalar.activation(parts[g, jt][:], acc[:], COPY, scale=scale_of[g, jt])
             if g > 0:
-                newest = waiting[-JT - 1]
-                older = waiting[0 : RUN_PARTS - 1] if g < G - 1 else [w for w in waiting if w is not newest]
-                add_transposed([newest] + older)
+                add_transposed(*[(g - 1, jt) for jt in reversed(range(JT))])
 
         def skip_pass(acc, nt, a):
-            for s, (codes, scales, first) in enumerate(q_wx[nt // 2, a]):
-                cols = slice(first + (nt % 2) * P, first + (nt % 2 + 1) * P)
+            codes, scales, origin = q_wx[nt // 2, a]
+            for s in range(2):
+                first = origin + s * HALF + nt % 2 * P
+                cols = slice(first, first + P)
                 nc.tensor.matmul_mx(
                     acc[:], lhsT=codes[:, cols].bitcast(FP8X4), lhsT_scale=scales[:, cols],
                     rhs=q_x[a][0][:].bitcast(FP8X4), rhs_scale=q_x[a][1][:],
@@ -206,32 +197,44 @@ def tile_list_interp_hl_res_kernel(
 
         on_vector, on_scalar = nc.vector.tensor_copy, nc.scalar.copy
 
-        for g in range(G - 1):
+        upper = [sbuf([P, N, PACK], BF16, f"upper{a}", after) for a, after in enumerate((None, "got_w1"))]
+        both0 = sbuf([P, 2, 2, HALF * PACK], BF16, "both0")
+        for g in range(G):
             gather_words(g)
-        upper0 = upper_halves(wx_raw[0], "upper0", on_vector)
-        gather_words(G - 1)
-        project(0, range(JT))
-        both0 = truncate(upper0[:], N, "both0")
-        subtract(half(wx_raw[0], 0), both0, N, 0)
-        subtract(half(wx_raw[0], 1), both0, N, HALF)
-        rounded0 = cast(x_raw[0], "rounded0", on_vector)
-        q_wx[0, 0], q_wx[1, 0] = quantise_split(both0, N, "q_wx0")
-        q_x[0] = quantise(rounded0, "q_x0", J, after="wx0")
+        project(0)
+        for h in range(2):
+            upper_halves(half(wx0, h), upper[0][:, h * HALF : (h + 1) * HALF, :], on_vector)
+        for h in range(2):
+            truncate(flat(upper[0][:, h * HALF : (h + 1) * HALF, :]), both0[:, h, 0, :])
+        for h in range(2):
+            subtract(half(wx0, h), both0, h)
+        rounded0 = cast(x0, "rounded0", on_vector)
+        codes, scales = quantise(both0[:].rearrange("p h s e -> p (h s e)"), "q_wx0", after="x0")
+        for h in range(2):
+            q_wx[h, 0] = codes, scales, h * N
+        q_x[0] = quantise(flat(rounded0[:]), "q_x0")
 
-        turn_weights(1, 0)
-        for g in range(1, G - 1):
-            project(g, range(JT))
-        upper1 = upper_halves(wx_raw[1], "upper1", on_scalar, after="got_w2")
-        project(G - 1, range(JT))
-        rounded1 = cast(x_raw[1], "rounded1", on_scalar, after="got_w3")
+        project(1)
+        for h in range(2):
+            upper_halves(wx1[h], upper[1][:, h * HALF : (h + 1) * HALF, :], on_scalar)
+            project(2 + h)
+        rounded1 = cast(x1, "rounded1", on_scalar, after="got_w3")
 
-        both01 = truncate(upper1[:, 0:HALF, :], HALF, "both01", after="x0")
-        both11 = truncate(upper1[:, HALF:N, :], HALF, "both11", after="rounded0")
-        subtract(half(wx_raw[1], 0), both01, HALF, 0)
-        subtract(half(wx_raw[1], 1), both11, HALF, 0)
-        [q_wx[0, 1]] = quantise_split(both01, HALF, "q_wx01")
-        [q_wx[1, 1]] = quantise_split(both11, HALF, "q_wx11")
-        q_x[1] = quantise(rounded1, "q_x1", J)
+        skip = [bank(nt, f"skip{nt}") for nt in range(NT)]
+        skip_pass(skip[0], 0, 0)
+        skip_pass(skip[1], 1, 0)
+        add_transposed((G - 1, 1), (G - 1, 0))
+        skip_pass(skip[2], 2, 0)
+        add_transposed((G - 1, 3), (G - 1, 2))
+        skip_pass(skip[3], 3, 0)
+
+        both1 = sbuf([P, 2, 2, HALF * PACK], BF16, "both1", after="rounded0")
+        truncate(flat(upper[1][:]).rearrange("p (h e) -> p h e", h=2), both1[:, :, 0, :])
+        for h in range(2):
+            subtract(wx1[h], both1, h)
+        for h in range(2):
+            q_wx[h, 1] = *quantise(both1[:, h, :, :].rearrange("p s e -> p (s e)"), f"q_wx1{h}"), 0
+        q_x[1] = quantise(flat(rounded1[:]), "q_x1")
 
         late = sbuf([P, 2 * NT * J], F32, "late", after="got_w3")
         base = [late[:, nt * J : (nt + 1) * J] for nt in range(NT)]
@@ -244,10 +247,8 @@ def tile_list_interp_hl_res_kernel(
             nc.scalar.copy(moved[:, cols], sums[nt][:])
             nc.gpsimd.tensor_tensor(base[nt], moved[:, cols], res_sb[:, nt, :], ALU.add)
 
-        skip = [bank(nt, f"skip{nt}") for nt in range(NT)]
-        for a in range(PASSES):
-            for nt in range(NT):
-                skip_pass(skip[nt], nt, a)
+        for nt in range(NT):
+            skip_pass(skip[nt], nt, 1)
         for nt in range(NT):
             nc.vector.tensor_tensor(done[nt], skip[nt][:], base[nt], ALU.add)
             nc.sync.dma_start(out[nt * P : (nt + 1) * P, :], done[nt])

@@ -88,18 +88,18 @@ def tile_list_interp_hl_res_kernel(
             nc.sync.dma_start(raw, rows.rearrange("(p t) c -> p t c", t=PACK))
             return raw
 
+        nc.gpsimd.memset(as_int32(w_s), 0)
         nc.gpsimd.memset(as_int32(tab_s)[:, 0 : T // 8], 0)
         nc.gpsimd.memset(iw_rows[:], 0.0)
         make_identity(nc, ident[:])
         nc.vector.memset(as_int32(tab_s)[:, T // 8 : T // 4], 0)
-        nc.vector.memset(as_int32(w_s), 0)
         nc.vector.memset(as_int32(got_s), 0)
         nc.sync.dma_start(offsets[:], offs)
         nc.sync.dma_start(as_int32(w_w), w_words[0].bitcast(I32))
         nc.sync.dma_start(as_int32(tab_s)[0:P:SPREAD, :], tab_scales[0].bitcast(I32))
         w_rows = w_scales[0].bitcast(I32).rearrange("(q r) c -> r q c", r=4)
         for r in range(4):
-            nc.sync.dma_start(as_int32(w_s)[r:P:QUAD, :], w_rows[r])
+            nc.scalar.dma_start(as_int32(w_s)[r:P:QUAD, :], w_rows[r])
         nc.sync.dma_start(as_int32(tab_w), tab_words[0].rearrange("p t i -> p (t i)").bitcast(I32))
         for g in range(2):
             load_rows(g)
@@ -236,9 +236,10 @@ def tile_list_interp_hl_res_kernel(
             q_wx[h, 1] = *quantise(both1[:, h, :, :].rearrange("p s e -> p (s e)"), f"q_wx1{h}"), 0
         q_x[1] = quantise(flat(rounded1[:]), "q_x1")
 
-        late = sbuf([P, 2 * NT * J], F32, "late", after="got_w3")
-        base = [late[:, nt * J : (nt + 1) * J] for nt in range(NT)]
-        done = [late[:, (NT + nt) * J : (NT + nt + 1) * J] for nt in range(NT)]
+        early = sbuf([P, NT // 2, J], F32, "early", after="rounded0")
+        late = sbuf([P, NT // 2, J], F32, "late", after="got_w3")
+        base = [(early, late)[nt // 2][:, nt % 2, :] for nt in range(NT)]
+        done = sbuf([P, NT, J], F32, "done")
         for nt in range(NT // 2):
             nc.vector.tensor_tensor(base[nt], sums[nt][:], res_sb[:, nt, :], ALU.add)
         moved = sbuf([P, NT * J], F32, "moved", after="x1")
@@ -250,5 +251,8 @@ def tile_list_interp_hl_res_kernel(
         for nt in range(NT):
             skip_pass(skip[nt], nt, 1)
         for nt in range(NT):
-            nc.vector.tensor_tensor(done[nt], skip[nt][:], base[nt], ALU.add)
-            nc.sync.dma_start(out[nt * P : (nt + 1) * P, :], done[nt])
+            pieces = 2 if nt == NT - 1 else 1
+            for piece in range(pieces):
+                cols = slice(piece * J // pieces, (piece + 1) * J // pieces)
+                nc.vector.tensor_tensor(done[:, nt, cols], skip[nt][:, cols], base[nt][:, cols], ALU.add)
+                nc.sync.dma_start(out[nt * P : (nt + 1) * P, cols], done[:, nt, cols])

@@ -27,6 +27,7 @@ QUAD = 32
 SPREAD = 8
 LIST_ROWS = 16
 RUN = 2
+SHARE = 128
 BLOCK = 8
 HI_MASK = 0xFFF0FFF0 - (1 << 32)
 
@@ -118,8 +119,9 @@ def tile_list_interp_hl_res_kernel(
             for r in range(4):
                 nc.sync.dma_start(plane[r:P:QUAD, :], as_int32(picked)[SPREAD * r : P : QUAD, :])
             if h == 0:
-                wx0 = load_pass(wx, 0, "wx0")
-        x0 = load_pass(x, 0, "x0")
+                x0 = [load_pass(x, 0, "x00", 0, HALF)]
+        wx0 = load_pass(wx, 0, "wx0")
+        x0.append(load_pass(x, 0, "x01", HALF, HALF))
         wx1 = []
         for h in range(2):
             wx1.append(load_pass(wx, 1, f"wx1{h}", h * HALF, HALF))
@@ -201,6 +203,8 @@ def tile_list_interp_hl_res_kernel(
         both0 = sbuf([P, 2, 2, HALF * PACK], BF16, "both0")
         for g in range(G):
             gather_words(g)
+        rounded0 = sbuf([P, J, PACK], BF16, "rounded0")
+        nc.gpsimd.tensor_copy(rounded0[:, 0:HALF, :], x0[0].rearrange("p t c -> p c t"))
         project(0)
         for h in range(2):
             upper_halves(half(wx0, h), upper[0][:, h * HALF : (h + 1) * HALF, :], on_vector)
@@ -208,15 +212,17 @@ def tile_list_interp_hl_res_kernel(
             truncate(flat(upper[0][:, h * HALF : (h + 1) * HALF, :]), both0[:, h, 0, :])
         for h in range(2):
             subtract(half(wx0, h), both0, h)
-        rounded0 = cast(x0, "rounded0", on_vector)
-        codes, scales = quantise(both0[:].rearrange("p h s e -> p (h s e)"), "q_wx0", after="x0")
+        on_vector(words_view(rounded0[:, HALF:J, :]), rows_view(x0[1]))
+        codes, scales = quantise(both0[:].rearrange("p h s e -> p (h s e)"), "q_wx0", after="x01")
         for h in range(2):
             q_wx[h, 0] = codes, scales, h * N
+        upper_halves(wx1[0][:, :, SHARE:HALF], upper[1][:, SHARE:HALF, :], on_vector)
         q_x[0] = quantise(flat(rounded0[:]), "q_x0")
 
         project(1)
         for h in range(2):
-            upper_halves(wx1[h], upper[1][:, h * HALF : (h + 1) * HALF, :], on_scalar)
+            width = (SHARE, HALF)[h]
+            upper_halves(wx1[h][:, :, 0:width], upper[1][:, h * HALF : h * HALF + width, :], on_scalar)
             project(2 + h)
         rounded1 = cast(x1, "rounded1", on_scalar, after="got_w3")
 

@@ -19,7 +19,6 @@ COPY = mybir.ActivationFunctionType.Copy
 
 P = 128
 PACK = 4
-PASSES = L // (P * PACK)
 JT = J // P
 NT = N // P
 HALF = N // 2
@@ -27,8 +26,9 @@ QUAD = 32
 SPREAD = 8
 LIST_ROWS = 16
 RUN = 2
-SHARE = 128
 BLOCK = 8
+ZEROED = 640
+JOINED = 2
 HI_MASK = 0xFFF0FFF0 - (1 << 32)
 
 
@@ -37,17 +37,23 @@ def tile_list_interp_hl_res_kernel(
 ):
     nc = tc.nc
 
-    def rows_view(ap):
-        return ap.rearrange("p t (c i) -> p c t i", i=RUN)
-
-    def words_view(ap):
-        return ap.rearrange("p (c i) t -> p c t i", i=RUN)
-
-    def flat(ap):
-        return ap.rearrange("p c t -> p (c t)")
-
     def as_int32(tile):
         return tile[:].bitcast(I32)
+
+    def loaded(raw, cols):
+        return raw[:, :, cols].rearrange("p t (c i) -> p c t i", i=RUN)
+
+    def woven(tile, first, width):
+        return tile[:, first * PACK : (first + width) * PACK].rearrange("p (c i t) -> p c t i", i=RUN, t=PACK)
+
+    def loaded_plain(raw, cols):
+        return raw[:, :, cols].rearrange("p t c -> p c t")
+
+    def woven_plain(tile, first, width):
+        return tile[:, first * PACK : (first + width) * PACK].rearrange("p (c t) -> p c t", t=PACK)
+
+    def tops(raw):
+        return raw.bitcast(BF16).rearrange("p t (c two) -> p t c two", two=2)[:, :, :, 1]
 
     with ExitStack() as ctx:
         held = ctx.enter_context(tc.tile_pool(name="held", bufs=1))
@@ -66,7 +72,7 @@ def tile_list_interp_hl_res_kernel(
         w_s = sbuf([P, N], U8, "w_s")
         ident = sbuf([P, P], F32, "ident")
         iw_rows = sbuf([P, P], F32, "iw_rows")
-        iw_cols = sbuf([P, 2 * JT], F32, "iw_cols")
+        iw_cols = sbuf([P, JT], F32, "iw_cols")
         got_s = sbuf([P, G * J], U8, "got_s")
         weights = (iw0, iw1, iw2, iw3)
         scale_of = {}
@@ -83,78 +89,37 @@ def tile_list_interp_hl_res_kernel(
             for jt in range(JT):
                 scale_of[g, jt] = cols[:, jt, 0:1]
 
-        def load_pass(src, a, name, first=0, width=N):
+        def load_piece(src, a, name, first, width):
             raw = sbuf([P, PACK * width], F32, name)[:].rearrange("p (t c) -> p t c", t=PACK)
             rows = src[a * P * PACK : (a + 1) * P * PACK, first : first + width]
             nc.sync.dma_start(raw, rows.rearrange("(p t) c -> p t c", t=PACK))
             return raw
 
-        nc.gpsimd.memset(as_int32(w_s), 0)
-        nc.gpsimd.memset(as_int32(tab_s)[:, 0 : T // 8], 0)
-        nc.gpsimd.memset(iw_rows[:], 0.0)
-        make_identity(nc, ident[:])
-        nc.vector.memset(as_int32(tab_s)[:, T // 8 : T // 4], 0)
-        nc.vector.memset(as_int32(got_s), 0)
-        nc.sync.dma_start(offsets[:], offs)
-        nc.sync.dma_start(as_int32(w_w), w_words[0].bitcast(I32))
-        nc.sync.dma_start(as_int32(tab_s)[0:P:SPREAD, :], tab_scales[0].bitcast(I32))
-        w_rows = w_scales[0].bitcast(I32).rearrange("(q r) c -> r q c", r=4)
-        for r in range(4):
-            nc.scalar.dma_start(as_int32(w_s)[r:P:QUAD, :], w_rows[r])
-        nc.sync.dma_start(as_int32(tab_w), tab_words[0].rearrange("p t i -> p (t i)").bitcast(I32))
-        for g in range(2):
-            load_rows(g)
-
-        iw_turned = bank(JT - 1, "iw_turned")
-        nc.tensor.transpose(iw_turned[:, 0:P], iw_rows[:], ident[:])
-        nc.scalar.activation(iw_cols[:], iw_turned[:, 0 : 2 * JT], COPY)
-
-        sums = [psum.tile([P, J], F32, name=f"sum{nt}") for nt in range(NT)]
-
-        for h in range(2):
-            picked = sbuf([P, 2 * J], U8, f"picked{h}")
+        def gather_scales(h, after=None):
+            picked = sbuf([P, 2 * J], U8, f"picked{h}", after)
             entries = offsets[:, 2 * h * J // LIST_ROWS : 2 * (h + 1) * J // LIST_ROWS]
             nc.vector.tensor_copy(picked[:], tab_s[:].indirect(entries))
+            return picked
+
+        def move_scales(h, picked):
             plane = as_int32(got_s)[:, h * J // 2 : (h + 1) * J // 2]
             for r in range(4):
                 nc.sync.dma_start(plane[r:P:QUAD, :], as_int32(picked)[SPREAD * r : P : QUAD, :])
-            if h == 0:
-                x0 = [load_pass(x, 0, "x00", 0, HALF)]
-        wx0 = load_pass(wx, 0, "wx0")
-        x0.append(load_pass(x, 0, "x01", HALF, HALF))
-        wx1 = []
-        for h in range(2):
-            wx1.append(load_pass(wx, 1, f"wx1{h}", h * HALF, HALF))
-            load_columns(2 + h)
-        x1 = load_pass(x, 1, "x1")
-        res_sb = sbuf([P, NT, J], F32, "res_sb")
-        nc.sync.dma_start(res_sb[:], res.rearrange("(nt p) j -> p nt j", p=P))
 
-        got_w, q_wx, q_x = {}, {}, {}
+        def truncate(upper, first, hi, place, width):
+            nc.vector.tensor_scalar(
+                hi[:, place * PACK : (place + width) * PACK].bitcast(I32),
+                upper[:, first * PACK : (first + width) * PACK].bitcast(I32), HI_MASK, None, ALU.bitwise_and,
+            )
 
-        def gather_words(g):
-            got_w[g] = sbuf([P, J], U32, f"got_w{g}")
-            entries = offsets[:, g * J // LIST_ROWS : (g + 1) * J // LIST_ROWS]
-            nc.vector.tensor_copy(got_w[g][:], tab_w[:].indirect(entries))
+        def subtract(raw, first, hi, lo, place, width):
+            nc.vector.tensor_tensor(
+                woven(lo, place, width), loaded(raw, slice(first, first + width)), woven(hi, place, width),
+                ALU.subtract,
+            )
 
-        def half(raw, h):
-            return raw[:, :, h * HALF : (h + 1) * HALF]
-
-        def upper_halves(raw, upper, copy):
-            tops = raw.bitcast(BF16).rearrange("p t (c two) -> p t c two", two=2)[:, :, :, 1]
-            copy(words_view(upper), rows_view(tops))
-
-        def truncate(upper, hi):
-            nc.vector.tensor_scalar(hi.bitcast(I32), upper.bitcast(I32), HI_MASK, None, ALU.bitwise_and)
-
-        def subtract(raw, both, h):
-            hi, lo = (both[:, h, s, :].rearrange("p (c t) -> p c t", t=PACK) for s in range(2))
-            nc.vector.tensor_tensor(words_view(lo), rows_view(raw), words_view(hi), ALU.subtract)
-
-        def cast(raw, name, copy, after=None):
-            rounded = sbuf([P, J, PACK], BF16, name, after)
-            copy(words_view(rounded[:]), rows_view(raw))
-            return rounded
+        def on_gpsimd(dst, src):
+            nc.gpsimd.tensor_scalar(dst, src, 1.0, 0.0, ALU.mult, ALU.add)
 
         def quantise(src, name, after=None):
             width = src.shape[1] // PACK
@@ -163,17 +128,87 @@ def tile_list_interp_hl_res_kernel(
             nc.vector.quantize_mx(out=codes[:].bitcast(FP8X4), scales=scales[:], in_=src)
             return codes, scales
 
+        nc.gpsimd.memset(as_int32(tab_s)[:, 0:ZEROED], 0)
+        nc.gpsimd.memset(as_int32(w_s), 0)
+        nc.gpsimd.memset(as_int32(got_s), 0)
+        nc.gpsimd.memset(iw_rows[:], 0.0)
+        make_identity(nc, ident[:])
+        nc.vector.memset(as_int32(tab_s)[:, ZEROED : T // 4], 0)
+        nc.sync.dma_start(offsets[:], offs)
+        nc.sync.dma_start(as_int32(tab_s)[0:P:SPREAD, :], tab_scales[0].bitcast(I32))
+        nc.sync.dma_start(as_int32(w_w), w_words[0].bitcast(I32))
+        w_rows = w_scales[0].bitcast(I32).rearrange("(q r) c -> r q c", r=4)
+        for r in range(4):
+            nc.scalar.dma_start(as_int32(w_s)[r:P:QUAD, :], w_rows[r])
+        wx0a = load_piece(wx, 0, "wx0a", 0, HALF)
+        nc.sync.dma_start(as_int32(tab_w), tab_words[0].rearrange("p t i -> p (t i)").bitcast(I32))
+        load_rows(0)
+
+        whole = slice(0, HALF)
+        hi = [sbuf([P, N * PACK], BF16, f"hi{a}") for a in range(2)]
+        lo = [sbuf([P, N * PACK], BF16, f"lo{a}") for a in range(2)]
+        upper0a = sbuf([P, HALF * PACK], BF16, "upper0a")
+        nc.scalar.copy(woven(upper0a, 0, HALF), loaded(tops(wx0a), whole))
+
+        iw_turned = bank(JT - 1, "iw_turned")
+        nc.tensor.transpose(iw_turned[:, 0:P], iw_rows[:], ident[:])
+        nc.scalar.activation(iw_cols[:], iw_turned[:, 0:JT], COPY)
+
+        move_scales(0, gather_scales(0))
+        truncate(upper0a, 0, hi[0], 0, HALF)
+        picked1 = gather_scales(1, after="upper0a")
+        nc.gpsimd.tensor_tensor(
+            woven_plain(lo[0], 0, HALF), loaded_plain(wx0a, whole), woven_plain(hi[0], 0, HALF), ALU.subtract
+        )
+        x0 = [load_piece(x, 0, "x0" + "ab"[h], h * HALF, HALF) for h in range(2)]
+        move_scales(1, picked1)
+        load_columns(1)
+        wx0b = load_piece(wx, 0, "wx0b", HALF, HALF)
+        x1 = []
+        for h in range(2):
+            x1.append(load_piece(x, 1, "x1" + "ab"[h], h * HALF, HALF))
+            load_columns(2 + h)
+        wx1 = load_piece(wx, 1, "wx1", 0, N)
+        res_sb = sbuf([P, NT, J], F32, "res_sb")
+        nc.sync.dma_start(res_sb[:], res.rearrange("(nt p) j -> p nt j", p=P))
+
+        got_w = {}
+        for g in range(G):
+            got_w[g] = sbuf([P, J], U32, f"got_w{g}")
+            entries = offsets[:, g * J // LIST_ROWS : (g + 1) * J // LIST_ROWS]
+            nc.vector.tensor_copy(got_w[g][:], tab_w[:].indirect(entries))
+
+        rounded = [sbuf([P, J * PACK], BF16, f"rounded{a}") for a in range(2)]
+        upper0b = sbuf([P, HALF * PACK], BF16, "upper0b")
+        for h in range(2):
+            on_gpsimd(woven_plain(rounded[0], h * HALF, HALF), loaded_plain(x0[h], whole))
+        on_gpsimd(woven_plain(upper0b, 0, P), loaded_plain(tops(wx0b), slice(0, P)))
+
+        q_x, q_hi, q_lo = {}, {}, {}
+        q_x[0] = quantise(rounded[0][:], "q_x0")
+        nc.vector.tensor_copy(woven(upper0b, P, P), loaded(tops(wx0b), slice(P, HALF)))
+        for i in range(2):
+            truncate(upper0b, i * P, hi[0], HALF + i * P, P)
+        for i in range(2):
+            subtract(wx0b, i * P, hi[0], lo[0], HALF + i * P, P)
+        q_hi[0] = quantise(hi[0][:], "q_hi0")
+        codes, scales = quantise(lo[0][:], "q_lo0")
+        for nt in range(NT):
+            q_lo[0, nt] = codes, scales, nt * P
+
+        sums = [psum.tile([P, J], F32, name=f"sum{nt}") for nt in range(NT)]
         parts = {}
 
-        def add_transposed(*tiles):
-            for g, jt in tiles:
-                for nt in range(NT):
-                    nc.tensor.matmul(
-                        sums[nt][:, jt * P : (jt + 1) * P], parts[g, jt][:, nt * P : (nt + 1) * P], ident[:],
-                        start=(g, jt) == (0, JT - 1), stop=(g, jt) == (G - 1, JT - 2), is_transpose=True,
-                    )
+        def add_transposed(g, jt, nt):
+            nc.tensor.matmul(
+                sums[nt][:, jt * P : (jt + 1) * P], parts[g, jt][:, nt * P : (nt + 1) * P], ident[:],
+                start=(g, jt) == (0, JT - 1), stop=(g, jt) == (G - 1, 0), is_transpose=True,
+            )
 
-        def project(g):
+        def project(g, after=None):
+            weighted = sbuf([P, JT * N], F32, f"part{g}", after)
+            if g == G - 1:
+                joined = sbuf([P, JOINED * N], F32, "joined", after="upper1a")
             for jt in range(JT):
                 acc = bank(jt, f"acc{g}_{jt}")
                 nc.tensor.matmul_mx(
@@ -181,84 +216,88 @@ def tile_list_interp_hl_res_kernel(
                     lhsT_scale=got_s[:, g * J + jt * P : g * J + (jt + 1) * P],
                     rhs=w_w[:].bitcast(FP4X4), rhs_scale=w_s[:], start=True, stop=True,
                 )
-                parts[g, jt] = sbuf([P, N], F32, f"part{g}_{jt}")
-                nc.scalar.activation(parts[g, jt][:], acc[:], COPY, scale=scale_of[g, jt])
+                if g == G - 1 and jt < JOINED:
+                    parts[g, jt] = joined[:, jt * N : (jt + 1) * N]
+                    nc.vector.scalar_tensor_tensor(
+                        parts[g, jt], acc[:], scale_of[g, jt], parts[g - 1, jt], ALU.mult, ALU.add
+                    )
+                else:
+                    parts[g, jt] = weighted[:, jt * N : (jt + 1) * N]
+                    nc.scalar.activation(parts[g, jt], acc[:], COPY, scale=scale_of[g, jt])
             if g > 0:
-                add_transposed(*[(g - 1, jt) for jt in reversed(range(JT))])
+                for jt in reversed(range(JOINED if g == G - 1 else 0, JT)):
+                    for nt in range(NT):
+                        add_transposed(g - 1, jt, nt)
 
-        def skip_pass(acc, nt, a):
-            codes, scales, origin = q_wx[nt // 2, a]
-            for s in range(2):
-                first = origin + s * HALF + nt % 2 * P
-                cols = slice(first, first + P)
-                nc.tensor.matmul_mx(
-                    acc[:], lhsT=codes[:, cols].bitcast(FP8X4), lhsT_scale=scales[:, cols],
-                    rhs=q_x[a][0][:].bitcast(FP8X4), rhs_scale=q_x[a][1][:],
-                    start=a == 0 and s == 0, stop=a == PASSES - 1 and s == 1,
-                )
+        def skip_pass(nt, a, codes, scales, first, start=False, stop=False):
+            cols = slice(first, first + P)
+            nc.tensor.matmul_mx(
+                skip[nt][:], lhsT=codes[:, cols].bitcast(FP8X4), lhsT_scale=scales[:, cols],
+                rhs=q_x[a][0][:].bitcast(FP8X4), rhs_scale=q_x[a][1][:], start=start, stop=stop,
+            )
 
-        on_vector, on_scalar = nc.vector.tensor_copy, nc.scalar.copy
-
-        upper = [sbuf([P, N, PACK], BF16, f"upper{a}", after) for a, after in enumerate((None, "got_w1"))]
-        both0 = sbuf([P, 2, 2, HALF * PACK], BF16, "both0")
-        for g in range(G):
-            gather_words(g)
-        rounded0 = sbuf([P, J, PACK], BF16, "rounded0")
-        nc.gpsimd.tensor_copy(rounded0[:, 0:HALF, :], x0[0].rearrange("p t c -> p c t"))
         project(0)
-        for h in range(2):
-            upper_halves(half(wx0, h), upper[0][:, h * HALF : (h + 1) * HALF, :], on_vector)
-        for h in range(2):
-            truncate(flat(upper[0][:, h * HALF : (h + 1) * HALF, :]), both0[:, h, 0, :])
-        for h in range(2):
-            subtract(half(wx0, h), both0, h)
-        on_vector(words_view(rounded0[:, HALF:J, :]), rows_view(x0[1]))
-        codes, scales = quantise(both0[:].rearrange("p h s e -> p (h s e)"), "q_wx0", after="x01")
-        for h in range(2):
-            q_wx[h, 0] = codes, scales, h * N
-        upper_halves(wx1[0][:, :, SHARE:HALF], upper[1][:, SHARE:HALF, :], on_vector)
-        q_x[0] = quantise(flat(rounded0[:]), "q_x0")
-
         project(1)
+        upper1 = [sbuf([P, HALF * PACK], BF16, "upper1" + "ab"[h]) for h in range(2)]
         for h in range(2):
-            width = (SHARE, HALF)[h]
-            upper_halves(wx1[h][:, :, 0:width], upper[1][:, h * HALF : h * HALF + width, :], on_scalar)
-            project(2 + h)
-        rounded1 = cast(x1, "rounded1", on_scalar, after="got_w3")
+            nc.vector.tensor_copy(woven(upper1[h], 0, HALF), loaded(tops(wx1), slice(h * HALF, (h + 1) * HALF)))
+        for h in range(2):
+            truncate(upper1[h], 0, hi[1], h * HALF, HALF)
+        for h in range(2):
+            nc.scalar.copy(woven(rounded[1], h * HALF, HALF), loaded(x1[h], whole))
+            project(2 + h, after="x1a")
+        subtract(wx1, 0, hi[1], lo[1], 0, HALF)
+        q_x[1] = quantise(rounded[1][:], "q_x1", after="upper1b")
+        q_hi[1] = quantise(hi[1][:], "q_hi1")
+        subtract(wx1, HALF, hi[1], lo[1], HALF, HALF)
+
+        def quantise_lo(h):
+            codes, scales = quantise(lo[1][:, h * HALF * PACK : (h + 1) * HALF * PACK], f"q_lo1{h}")
+            for i in range(2):
+                q_lo[1, 2 * h + i] = codes, scales, i * P
 
         skip = [bank(nt, f"skip{nt}") for nt in range(NT)]
-        skip_pass(skip[0], 0, 0)
-        skip_pass(skip[1], 1, 0)
-        add_transposed((G - 1, 1), (G - 1, 0))
-        skip_pass(skip[2], 2, 0)
-        add_transposed((G - 1, 3), (G - 1, 2))
-        skip_pass(skip[3], 3, 0)
 
-        both1 = sbuf([P, 2, 2, HALF * PACK], BF16, "both1", after="rounded0")
-        truncate(flat(upper[1][:]).rearrange("p (h e) -> p h e", h=2), both1[:, :, 0, :])
-        for h in range(2):
-            subtract(wx1[h], both1, h)
-        for h in range(2):
-            q_wx[h, 1] = *quantise(both1[:, h, :, :].rearrange("p s e -> p (s e)"), f"q_wx1{h}"), 0
-        q_x[1] = quantise(flat(rounded1[:]), "q_x1")
+        def first_passes(nt):
+            skip_pass(nt, 0, *q_hi[0], nt * P, start=True)
+            skip_pass(nt, 0, *q_lo[0, nt])
 
-        early = sbuf([P, NT // 2, J], F32, "early", after="rounded0")
-        late = sbuf([P, NT // 2, J], F32, "late", after="got_w3")
-        base = [(early, late)[nt // 2][:, nt % 2, :] for nt in range(NT)]
-        done = sbuf([P, NT, J], F32, "done")
-        for nt in range(NT // 2):
-            nc.vector.tensor_tensor(base[nt], sums[nt][:], res_sb[:, nt, :], ALU.add)
-        moved = sbuf([P, NT * J], F32, "moved", after="x1")
-        for nt in range(NT // 2, NT):
-            cols = slice(nt * J, (nt + 1) * J)
-            nc.scalar.copy(moved[:, cols], sums[nt][:])
-            nc.gpsimd.tensor_tensor(base[nt], moved[:, cols], res_sb[:, nt, :], ALU.add)
+        def last_passes(nt):
+            skip_pass(nt, 1, *q_hi[1], nt * P)
+            skip_pass(nt, 1, *q_lo[1, nt], stop=True)
+
+        for nt in range(NT - 1):
+            first_passes(nt)
+        for nt in range(NT):
+            for jt in reversed(range(JT)):
+                add_transposed(G - 1, jt, nt)
+
+        base = sbuf([P, NT * J], F32, "base")
+        late = sbuf([P, NT // 2 * J], F32, "late", after="lo1")
+        moved = sbuf([P, NT // 2 * J], F32, "moved")
+        done = sbuf([P, NT * J], F32, "done")
+
+        quantise_lo(0)
+        quantise_lo(1)
+        bases = []
+        for nt in range(NT):
+            if nt < NT // 2:
+                bases.append(base[:, nt * J : (nt + 1) * J])
+                nc.vector.tensor_tensor(bases[nt], sums[nt][:], res_sb[:, nt, :], ALU.add)
+            else:
+                cols = slice((nt - NT // 2) * J, (nt - NT // 2 + 1) * J)
+                bases.append(late[:, cols])
+                nc.scalar.copy(moved[:, cols], sums[nt][:])
+                nc.gpsimd.tensor_tensor(bases[nt], moved[:, cols], res_sb[:, nt, :], ALU.add)
 
         for nt in range(NT):
-            skip_pass(skip[nt], nt, 1)
+            if nt == NT - 1:
+                first_passes(nt)
+            last_passes(nt)
         for nt in range(NT):
             pieces = 2 if nt == NT - 1 else 1
             for piece in range(pieces):
                 cols = slice(piece * J // pieces, (piece + 1) * J // pieces)
-                nc.vector.tensor_tensor(done[:, nt, cols], skip[nt][:, cols], base[nt][:, cols], ALU.add)
-                nc.sync.dma_start(out[nt * P : (nt + 1) * P, cols], done[:, nt, cols])
+                place = slice(nt * J + cols.start, nt * J + cols.stop)
+                nc.vector.tensor_tensor(done[:, place], skip[nt][:, cols], bases[nt][:, cols], ALU.add)
+                nc.sync.dma_start(out[nt * P : (nt + 1) * P, cols], done[:, place])

@@ -22,13 +22,12 @@ PACK = 4
 JT = J // P
 NT = N // P
 HALF = N // 2
+SPAN = HALF * PACK
 QUAD = 32
 SPREAD = 8
 LIST_ROWS = 16
 RUN = 2
 BLOCK = 8
-ZEROED = 640
-JOINED = 2
 HI_MASK = 0xFFF0FFF0 - (1 << 32)
 
 
@@ -40,17 +39,17 @@ def tile_list_interp_hl_res_kernel(
     def as_int32(tile):
         return tile[:].bitcast(I32)
 
-    def loaded(raw, cols):
-        return raw[:, :, cols].rearrange("p t (c i) -> p c t i", i=RUN)
+    def loaded(raw):
+        return raw.rearrange("p t (c i) -> p c t i", i=RUN)
 
-    def woven(tile, first, width):
-        return tile[:, first * PACK : (first + width) * PACK].rearrange("p (c i t) -> p c t i", i=RUN, t=PACK)
+    def woven(run):
+        return run.rearrange("p (c i t) -> p c t i", i=RUN, t=PACK)
 
-    def loaded_plain(raw, cols):
-        return raw[:, :, cols].rearrange("p t c -> p c t")
+    def loaded_plain(raw):
+        return raw.rearrange("p t c -> p c t")
 
-    def woven_plain(tile, first, width):
-        return tile[:, first * PACK : (first + width) * PACK].rearrange("p (c t) -> p c t", t=PACK)
+    def woven_plain(run):
+        return run.rearrange("p (c t) -> p c t", t=PACK)
 
     def tops(raw):
         return raw.bitcast(BF16).rearrange("p t (c two) -> p t c two", two=2)[:, :, :, 1]
@@ -72,22 +71,23 @@ def tile_list_interp_hl_res_kernel(
         w_s = sbuf([P, N], U8, "w_s")
         ident = sbuf([P, P], F32, "ident")
         iw_rows = sbuf([P, P], F32, "iw_rows")
-        iw_cols = sbuf([P, JT], F32, "iw_cols")
+        iw_cols = sbuf([P, 2 * JT], F32, "iw_cols")
         got_s = sbuf([P, G * J], U8, "got_s")
         weights = (iw0, iw1, iw2, iw3)
         scale_of = {}
 
-        def load_rows(g):
-            nc.sync.dma_start(iw_rows[g * JT : (g + 1) * JT, :], weights[g].rearrange("(jt p) -> jt p", p=P))
-            for jt in range(JT):
+        def load_rows(g, count):
+            rows = weights[g].rearrange("(jt p) -> jt p", p=P)
+            nc.sync.dma_start(iw_rows[g * JT : g * JT + count, :], rows[0:count, :])
+            for jt in range(count):
                 scale_of[g, jt] = iw_cols[:, g * JT + jt : g * JT + jt + 1]
 
-        def load_columns(g):
-            cols = sbuf([P, JT, BLOCK], F32, f"iw_cols{g}")
+        def load_columns(g, first):
+            cols = sbuf([P, JT - first, BLOCK], F32, f"iw_cols{g}")
             with nc.allow_non_contiguous_dma(reason="one weight a partition and tile"):
-                nc.sync.dma_start(cols[:, :, 0], weights[g].rearrange("(jt p) -> p jt", p=P))
-            for jt in range(JT):
-                scale_of[g, jt] = cols[:, jt, 0:1]
+                nc.sync.dma_start(cols[:, :, 0], weights[g].rearrange("(jt p) -> p jt", p=P)[:, first:JT])
+            for jt in range(first, JT):
+                scale_of[g, jt] = cols[:, jt - first, 0:1]
 
         def load_piece(src, a, name, first, width):
             raw = sbuf([P, PACK * width], F32, name)[:].rearrange("p (t c) -> p t c", t=PACK)
@@ -106,69 +106,62 @@ def tile_list_interp_hl_res_kernel(
             for r in range(4):
                 nc.sync.dma_start(plane[r:P:QUAD, :], as_int32(picked)[SPREAD * r : P : QUAD, :])
 
-        def truncate(upper, first, hi, place, width):
-            nc.vector.tensor_scalar(
-                hi[:, place * PACK : (place + width) * PACK].bitcast(I32),
-                upper[:, first * PACK : (first + width) * PACK].bitcast(I32), HI_MASK, None, ALU.bitwise_and,
-            )
+        def truncate(upper, hi):
+            nc.vector.tensor_scalar(hi.bitcast(I32), upper.bitcast(I32), HI_MASK, None, ALU.bitwise_and)
 
-        def subtract(raw, first, hi, lo, place, width):
-            nc.vector.tensor_tensor(
-                woven(lo, place, width), loaded(raw, slice(first, first + width)), woven(hi, place, width),
-                ALU.subtract,
-            )
+        def subtract(raw, both):
+            nc.vector.tensor_tensor(woven(both[:, SPAN : 2 * SPAN]), loaded(raw), woven(both[:, 0:SPAN]), ALU.subtract)
 
-        def on_gpsimd(dst, src):
-            nc.gpsimd.tensor_scalar(dst, src, 1.0, 0.0, ALU.mult, ALU.add)
+        def coded(width, name, after=None):
+            return sbuf([P, width], U32, name + "_codes", after), sbuf([P, width], U8, name + "_scales")
+
+        def quantise_into(target, first, src):
+            cols = slice(first, first + src.shape[1] // PACK)
+            nc.vector.quantize_mx(out=target[0][:, cols].bitcast(FP8X4), scales=target[1][:, cols], in_=src)
 
         def quantise(src, name, after=None):
-            width = src.shape[1] // PACK
-            codes = sbuf([P, width], U32, name + "_codes", after)
-            scales = sbuf([P, width], U8, name + "_scales")
-            nc.vector.quantize_mx(out=codes[:].bitcast(FP8X4), scales=scales[:], in_=src)
-            return codes, scales
+            target = coded(src.shape[1] // PACK, name, after)
+            quantise_into(target, 0, src)
+            return target
 
-        nc.gpsimd.memset(as_int32(tab_s)[:, 0:ZEROED], 0)
         nc.gpsimd.memset(as_int32(w_s), 0)
-        nc.gpsimd.memset(as_int32(got_s), 0)
+        nc.gpsimd.memset(as_int32(tab_s)[:, 0 : T // 8], 0)
         nc.gpsimd.memset(iw_rows[:], 0.0)
         make_identity(nc, ident[:])
-        nc.vector.memset(as_int32(tab_s)[:, ZEROED : T // 4], 0)
+        nc.vector.memset(as_int32(tab_s)[:, T // 8 : T // 4], 0)
+        nc.vector.memset(as_int32(got_s), 0)
         nc.sync.dma_start(offsets[:], offs)
-        nc.sync.dma_start(as_int32(tab_s)[0:P:SPREAD, :], tab_scales[0].bitcast(I32))
         nc.sync.dma_start(as_int32(w_w), w_words[0].bitcast(I32))
+        nc.sync.dma_start(as_int32(tab_s)[0:P:SPREAD, :], tab_scales[0].bitcast(I32))
         w_rows = w_scales[0].bitcast(I32).rearrange("(q r) c -> r q c", r=4)
         for r in range(4):
             nc.scalar.dma_start(as_int32(w_s)[r:P:QUAD, :], w_rows[r])
         wx0a = load_piece(wx, 0, "wx0a", 0, HALF)
         nc.sync.dma_start(as_int32(tab_w), tab_words[0].rearrange("p t i -> p (t i)").bitcast(I32))
-        load_rows(0)
+        load_rows(0, JT)
+        load_rows(1, JT - 1)
 
-        whole = slice(0, HALF)
-        hi = [sbuf([P, N * PACK], BF16, f"hi{a}") for a in range(2)]
-        lo = [sbuf([P, N * PACK], BF16, f"lo{a}") for a in range(2)]
-        upper0a = sbuf([P, HALF * PACK], BF16, "upper0a")
-        nc.scalar.copy(woven(upper0a, 0, HALF), loaded(tops(wx0a), whole))
-
+        both0 = [sbuf([P, 2 * SPAN], BF16, "both0" + "ab"[h]) for h in range(2)]
+        upper0a = sbuf([P, SPAN], BF16, "upper0a")
+        nc.scalar.copy(woven(upper0a[:]), loaded(tops(wx0a)))
         iw_turned = bank(JT - 1, "iw_turned")
         nc.tensor.transpose(iw_turned[:, 0:P], iw_rows[:], ident[:])
-        nc.scalar.activation(iw_cols[:], iw_turned[:, 0:JT], COPY)
+        nc.scalar.activation(iw_cols[:], iw_turned[:, 0 : 2 * JT], COPY)
 
         move_scales(0, gather_scales(0))
-        truncate(upper0a, 0, hi[0], 0, HALF)
+        truncate(upper0a[:], both0[0][:, 0:SPAN])
         picked1 = gather_scales(1, after="upper0a")
         nc.gpsimd.tensor_tensor(
-            woven_plain(lo[0], 0, HALF), loaded_plain(wx0a, whole), woven_plain(hi[0], 0, HALF), ALU.subtract
+            woven_plain(both0[0][:, SPAN : 2 * SPAN]), loaded_plain(wx0a), woven_plain(both0[0][:, 0:SPAN]), ALU.subtract
         )
         x0 = [load_piece(x, 0, "x0" + "ab"[h], h * HALF, HALF) for h in range(2)]
-        move_scales(1, picked1)
-        load_columns(1)
         wx0b = load_piece(wx, 0, "wx0b", HALF, HALF)
-        x1 = []
-        for h in range(2):
-            x1.append(load_piece(x, 1, "x1" + "ab"[h], h * HALF, HALF))
-            load_columns(2 + h)
-        wx1 = load_piece(wx, 1, "wx1", 0, N)
+        move_scales(1, picked1)
+        load_columns(1, JT - 1)
+        load_columns(2, 0)
+        wx1 = [load_piece(wx, 1, "wx1" + "ab"[h], h * HALF, HALF) for h in range(2)]
+        load_columns(3, 0)
+        x1 = load_piece(x, 1, "x1", 0, J)
         res_sb = sbuf([P, NT, J], F32, "res_sb")
         nc.sync.dma_start(res_sb[:], res.rearrange("(nt p) j -> p nt j", p=P))
 
@@ -178,37 +171,30 @@ def tile_list_interp_hl_res_kernel(
             entries = offsets[:, g * J // LIST_ROWS : (g + 1) * J // LIST_ROWS]
             nc.vector.tensor_copy(got_w[g][:], tab_w[:].indirect(entries))
 
-        rounded = [sbuf([P, J * PACK], BF16, f"rounded{a}") for a in range(2)]
-        upper0b = sbuf([P, HALF * PACK], BF16, "upper0b")
-        for h in range(2):
-            on_gpsimd(woven_plain(rounded[0], h * HALF, HALF), loaded_plain(x0[h], whole))
-        on_gpsimd(woven_plain(upper0b, 0, P), loaded_plain(tops(wx0b), slice(0, P)))
+        rounded0a = sbuf([P, SPAN], BF16, "rounded0a")
+        nc.gpsimd.tensor_scalar(woven_plain(rounded0a[:]), loaded_plain(x0[0]), 1.0, 0.0, ALU.mult, ALU.add)
 
-        q_x, q_hi, q_lo = {}, {}, {}
-        q_x[0] = quantise(rounded[0][:], "q_x0")
-        nc.vector.tensor_copy(woven(upper0b, P, P), loaded(tops(wx0b), slice(P, HALF)))
-        for i in range(2):
-            truncate(upper0b, i * P, hi[0], HALF + i * P, P)
-        for i in range(2):
-            subtract(wx0b, i * P, hi[0], lo[0], HALF + i * P, P)
-        q_hi[0] = quantise(hi[0][:], "q_hi0")
-        codes, scales = quantise(lo[0][:], "q_lo0")
-        for nt in range(NT):
-            q_lo[0, nt] = codes, scales, nt * P
+        q_wx, q_x = {}, {}
+        rest0 = sbuf([P, 2 * SPAN], BF16, "rest0", after="upper0a")
+        upper0b, rounded0b = rest0[:, 0:SPAN], rest0[:, SPAN : 2 * SPAN]
+        nc.vector.tensor_copy(woven(upper0b), loaded(tops(wx0b)))
+        nc.vector.tensor_copy(woven(rounded0b), loaded(x0[1]))
+        truncate(upper0b, both0[1][:, 0:SPAN])
+        q_wx[0, 0] = quantise(both0[0][:], "q_wx0a", after="x0b")
+        subtract(wx0b, both0[1][:])
 
         sums = [psum.tile([P, J], F32, name=f"sum{nt}") for nt in range(NT)]
         parts = {}
 
-        def add_transposed(g, jt, nt):
-            nc.tensor.matmul(
-                sums[nt][:, jt * P : (jt + 1) * P], parts[g, jt][:, nt * P : (nt + 1) * P], ident[:],
-                start=(g, jt) == (0, JT - 1), stop=(g, jt) == (G - 1, 0), is_transpose=True,
-            )
+        def add_transposed(g, tiles, rows=range(NT)):
+            for jt in tiles:
+                for nt in rows:
+                    nc.tensor.matmul(
+                        sums[nt][:, jt * P : (jt + 1) * P], parts[g, jt][:, nt * P : (nt + 1) * P], ident[:],
+                        start=(g, jt) == (0, 1), stop=(g, jt) == (G - 1, JT - 2), is_transpose=True,
+                    )
 
-        def project(g, after=None):
-            weighted = sbuf([P, JT * N], F32, f"part{g}", after)
-            if g == G - 1:
-                joined = sbuf([P, JOINED * N], F32, "joined", after="upper1a")
+        for g in range(G):
             for jt in range(JT):
                 acc = bank(jt, f"acc{g}_{jt}")
                 nc.tensor.matmul_mx(
@@ -216,88 +202,72 @@ def tile_list_interp_hl_res_kernel(
                     lhsT_scale=got_s[:, g * J + jt * P : g * J + (jt + 1) * P],
                     rhs=w_w[:].bitcast(FP4X4), rhs_scale=w_s[:], start=True, stop=True,
                 )
-                if g == G - 1 and jt < JOINED:
-                    parts[g, jt] = joined[:, jt * N : (jt + 1) * N]
-                    nc.vector.scalar_tensor_tensor(
-                        parts[g, jt], acc[:], scale_of[g, jt], parts[g - 1, jt], ALU.mult, ALU.add
-                    )
-                else:
-                    parts[g, jt] = weighted[:, jt * N : (jt + 1) * N]
-                    nc.scalar.activation(parts[g, jt], acc[:], COPY, scale=scale_of[g, jt])
-            if g > 0:
-                for jt in reversed(range(JOINED if g == G - 1 else 0, JT)):
-                    for nt in range(NT):
-                        add_transposed(g - 1, jt, nt)
+                parts[g, jt] = sbuf([P, N], F32, f"part{g}_{jt}")
+                nc.scalar.activation(parts[g, jt][:], acc[:], COPY, scale=scale_of[g, jt])
+                if g == 1 and jt % 2 == 1:
+                    add_transposed(0, (jt, jt - 1))
+            if g > 1:
+                add_transposed(g - 1, reversed(range(JT)))
+        rounded1 = sbuf([P, 2 * SPAN], BF16, "rounded1", after="got_w2")
+        nc.scalar.copy(woven(rounded1[:]), loaded(x1))
 
-        def skip_pass(nt, a, codes, scales, first, start=False, stop=False):
-            cols = slice(first, first + P)
-            nc.tensor.matmul_mx(
-                skip[nt][:], lhsT=codes[:, cols].bitcast(FP8X4), lhsT_scale=scales[:, cols],
-                rhs=q_x[a][0][:].bitcast(FP8X4), rhs_scale=q_x[a][1][:], start=start, stop=stop,
-            )
-
-        project(0)
-        project(1)
-        upper1 = [sbuf([P, HALF * PACK], BF16, "upper1" + "ab"[h]) for h in range(2)]
+        upper1 = sbuf([P, 2 * SPAN], BF16, "upper1")
+        both1 = sbuf([P, 4 * SPAN], BF16, "both1")
+        nc.vector.tensor_copy(woven(upper1[:, 0:SPAN]), loaded(tops(wx1[0])))
+        q_wx[1, 0] = quantise(both0[1][:], "q_wx0b", after="part1_0")
+        nc.vector.tensor_copy(woven(upper1[:, SPAN : 2 * SPAN]), loaded(tops(wx1[1])))
+        q_x[0] = coded(J, "q_x0", after="both0b")
+        quantise_into(q_x[0], 0, rounded0a[:])
+        truncate(
+            upper1[:].rearrange("p (h e) -> p h e", h=2), both1[:].rearrange("p (h s e) -> p h s e", h=2, s=2)[:, :, 0, :]
+        )
+        quantise_into(q_x[0], HALF, rounded0b)
         for h in range(2):
-            nc.vector.tensor_copy(woven(upper1[h], 0, HALF), loaded(tops(wx1), slice(h * HALF, (h + 1) * HALF)))
+            subtract(wx1[h], both1[:, 2 * h * SPAN : 2 * (h + 1) * SPAN])
         for h in range(2):
-            truncate(upper1[h], 0, hi[1], h * HALF, HALF)
-        for h in range(2):
-            nc.scalar.copy(woven(rounded[1], h * HALF, HALF), loaded(x1[h], whole))
-            project(2 + h, after="x1a")
-        subtract(wx1, 0, hi[1], lo[1], 0, HALF)
-        q_x[1] = quantise(rounded[1][:], "q_x1", after="upper1b")
-        q_hi[1] = quantise(hi[1][:], "q_hi1")
-        subtract(wx1, HALF, hi[1], lo[1], HALF, HALF)
-
-        def quantise_lo(h):
-            codes, scales = quantise(lo[1][:, h * HALF * PACK : (h + 1) * HALF * PACK], f"q_lo1{h}")
-            for i in range(2):
-                q_lo[1, 2 * h + i] = codes, scales, i * P
+            q_wx[h, 1] = quantise(both1[:, 2 * h * SPAN : 2 * (h + 1) * SPAN], "q_wx1" + "ab"[h])
+        q_x[1] = quantise(rounded1[:], "q_x1")
 
         skip = [bank(nt, f"skip{nt}") for nt in range(NT)]
 
-        def first_passes(nt):
-            skip_pass(nt, 0, *q_hi[0], nt * P, start=True)
-            skip_pass(nt, 0, *q_lo[0, nt])
+        def skip_pass(nt, a):
+            codes, scales = q_wx[nt // 2, a]
+            for s in range(2):
+                cols = slice(s * HALF + nt % 2 * P, s * HALF + (nt % 2 + 1) * P)
+                nc.tensor.matmul_mx(
+                    skip[nt][:], lhsT=codes[:, cols].bitcast(FP8X4), lhsT_scale=scales[:, cols],
+                    rhs=q_x[a][0][:].bitcast(FP8X4), rhs_scale=q_x[a][1][:],
+                    start=a == 0 and s == 0, stop=a == 1 and s == 1,
+                )
 
-        def last_passes(nt):
-            skip_pass(nt, 1, *q_hi[1], nt * P)
-            skip_pass(nt, 1, *q_lo[1, nt], stop=True)
+        skip_pass(0, 0)
+        add_transposed(G - 1, (1, 0))
+        skip_pass(1, 0)
+        for nt in (2, 3, 0, 1):
+            add_transposed(G - 1, (3, 2), rows=[nt])
+        skip_pass(2, 0)
+        skip_pass(3, 0)
 
-        for nt in range(NT - 1):
-            first_passes(nt)
-        for nt in range(NT):
-            for jt in reversed(range(JT)):
-                add_transposed(G - 1, jt, nt)
-
-        base = sbuf([P, NT * J], F32, "base")
-        late = sbuf([P, NT // 2 * J], F32, "late", after="lo1")
-        moved = sbuf([P, NT // 2 * J], F32, "moved")
+        bases = sbuf([P, NT * J], F32, "bases", after="got_w2")
+        base = [bases[:, nt * J : (nt + 1) * J] for nt in range(NT)]
+        moved = sbuf([P, NT // 2 * J], F32, "moved", after="x1")
         done = sbuf([P, NT * J], F32, "done")
-
-        quantise_lo(0)
-        quantise_lo(1)
-        bases = []
-        for nt in range(NT):
-            if nt < NT // 2:
-                bases.append(base[:, nt * J : (nt + 1) * J])
-                nc.vector.tensor_tensor(bases[nt], sums[nt][:], res_sb[:, nt, :], ALU.add)
-            else:
-                cols = slice((nt - NT // 2) * J, (nt - NT // 2 + 1) * J)
-                bases.append(late[:, cols])
-                nc.scalar.copy(moved[:, cols], sums[nt][:])
-                nc.gpsimd.tensor_tensor(bases[nt], moved[:, cols], res_sb[:, nt, :], ALU.add)
+        for nt in range(NT // 2):
+            nc.vector.tensor_tensor(base[nt], sums[nt][:], res_sb[:, nt, :], ALU.add)
+        for nt in range(NT // 2, NT):
+            copied = moved[:, (nt - NT // 2) * J : (nt - NT // 2 + 1) * J]
+            nc.scalar.copy(copied, sums[nt][:])
+            pieces = 2 if nt == NT - 1 else 1
+            for piece in range(pieces):
+                part = slice(piece * J // pieces, (piece + 1) * J // pieces)
+                nc.gpsimd.tensor_tensor(base[nt][:, part], copied[:, part], res_sb[:, nt, part], ALU.add)
 
         for nt in range(NT):
-            if nt == NT - 1:
-                first_passes(nt)
-            last_passes(nt)
+            skip_pass(nt, 1)
         for nt in range(NT):
             pieces = 2 if nt == NT - 1 else 1
             for piece in range(pieces):
                 cols = slice(piece * J // pieces, (piece + 1) * J // pieces)
                 place = slice(nt * J + cols.start, nt * J + cols.stop)
-                nc.vector.tensor_tensor(done[:, place], skip[nt][:, cols], bases[nt][:, cols], ALU.add)
+                nc.vector.tensor_tensor(done[:, place], skip[nt][:, cols], base[nt][:, cols], ALU.add)
                 nc.sync.dma_start(out[nt * P : (nt + 1) * P, cols], done[:, place])

@@ -24,7 +24,7 @@ NT = N // P
 HALF = N // 2
 SPAN = HALF * PACK
 QUAD = 32
-SPREAD = 8
+FIRST_ROW = P - 16
 LIST_ROWS = 16
 RUN = 2
 BLOCK = 8
@@ -56,7 +56,11 @@ def tile_list_interp_hl_res_kernel(
 
     with ExitStack() as ctx:
         held = ctx.enter_context(tc.tile_pool(name="held", bufs=1))
+        laid = ctx.enter_context(tc.tile_pool(name="laid", bufs=1))
         psum = ctx.enter_context(tc.psum_pool(name="psum", bufs=1))
+
+        def placed(shape, dtype, name, offset):
+            return laid.tile(shape, dtype, name=name, offset=offset, align_bytes=64)
 
         def sbuf(shape, dtype, name, after=None):
             return held.tile(shape, dtype, name=name, tag=after or name, align_bytes=64)
@@ -95,8 +99,7 @@ def tile_list_interp_hl_res_kernel(
             nc.sync.dma_start(raw, rows.rearrange("(p t) c -> p t c", t=PACK))
             return raw
 
-        def gather_scales(h, after=None):
-            picked = sbuf([P, 2 * J], U8, f"picked{h}", after)
+        def gather_scales(h, picked):
             entries = offsets[:, 2 * h * J // LIST_ROWS : 2 * (h + 1) * J // LIST_ROWS]
             nc.vector.tensor_copy(picked[:], tab_s[:].indirect(entries))
             return picked
@@ -104,7 +107,7 @@ def tile_list_interp_hl_res_kernel(
         def move_scales(h, picked):
             plane = as_int32(got_s)[:, h * J // 2 : (h + 1) * J // 2]
             for r in range(4):
-                nc.sync.dma_start(plane[r:P:QUAD, :], as_int32(picked)[SPREAD * r : P : QUAD, :])
+                nc.sync.dma_start(plane[r:P:QUAD, :], as_int32(picked)[FIRST_ROW + r : P : 4, :])
 
         def truncate(upper, hi):
             nc.vector.tensor_scalar(hi.bitcast(I32), upper.bitcast(I32), HI_MASK, None, ALU.bitwise_and)
@@ -124,40 +127,40 @@ def tile_list_interp_hl_res_kernel(
             quantise_into(target, 0, src)
             return target
 
-        nc.gpsimd.memset(as_int32(w_s), 0)
-        nc.gpsimd.memset(as_int32(tab_s)[:, 0 : T // 8], 0)
         nc.gpsimd.memset(iw_rows[:], 0.0)
+        nc.gpsimd.memset(as_int32(tab_s)[0:FIRST_ROW, 0 : T // 8], 0)
         make_identity(nc, ident[:])
-        nc.vector.memset(as_int32(tab_s)[:, T // 8 : T // 4], 0)
+        nc.vector.memset(as_int32(w_s), 0)
+        nc.vector.memset(as_int32(tab_s)[0:FIRST_ROW, T // 8 : T // 4], 0)
         nc.vector.memset(as_int32(got_s), 0)
+        w_rows = sbuf([4, 4, N // 4], I32, "w_rows")
+        nc.sync.dma_start(w_rows[:], w_scales[0].bitcast(I32).rearrange("(q r) c -> r q c", r=4))
+        nc.sync.dma_start(as_int32(tab_s)[FIRST_ROW:P, :], tab_scales[0].bitcast(I32))
         nc.sync.dma_start(offsets[:], offs)
-        nc.sync.dma_start(as_int32(w_w), w_words[0].bitcast(I32))
-        nc.sync.dma_start(as_int32(tab_s)[0:P:SPREAD, :], tab_scales[0].bitcast(I32))
-        w_rows = w_scales[0].bitcast(I32).rearrange("(q r) c -> r q c", r=4)
-        for r in range(4):
-            nc.scalar.dma_start(as_int32(w_s)[r:P:QUAD, :], w_rows[r])
+        for q in range(4):
+            nc.vector.tensor_copy(as_int32(w_s)[q * QUAD : q * QUAD + 4, :], w_rows[:, q, :])
         wx0a = load_piece(wx, 0, "wx0a", 0, HALF)
-        nc.sync.dma_start(as_int32(tab_w), tab_words[0].rearrange("p t i -> p (t i)").bitcast(I32))
         load_rows(0, JT)
-        load_rows(1, JT - 1)
+        load_rows(1, JT)
+        nc.sync.dma_start(as_int32(tab_w), tab_words[0].rearrange("p t i -> p (t i)").bitcast(I32))
+        nc.sync.dma_start(as_int32(w_w), w_words[0].bitcast(I32))
 
         both0 = [sbuf([P, 2 * SPAN], BF16, "both0" + "ab"[h]) for h in range(2)]
-        upper0a = sbuf([P, SPAN], BF16, "upper0a")
+        upper0a = placed([P, SPAN], BF16, "upper0a", 2 * SPAN)
         nc.scalar.copy(woven(upper0a[:]), loaded(tops(wx0a)))
         iw_turned = bank(JT - 1, "iw_turned")
         nc.tensor.transpose(iw_turned[:, 0:P], iw_rows[:], ident[:])
         nc.scalar.activation(iw_cols[:], iw_turned[:, 0 : 2 * JT], COPY)
 
-        move_scales(0, gather_scales(0))
+        move_scales(0, gather_scales(0, sbuf([P, 2 * J], U8, "picked0")))
         truncate(upper0a[:], both0[0][:, 0:SPAN])
-        picked1 = gather_scales(1, after="upper0a")
+        picked1 = gather_scales(1, placed([P, 2 * J], U8, "picked1", 4 * SPAN - J))
         nc.gpsimd.tensor_tensor(
             woven_plain(both0[0][:, SPAN : 2 * SPAN]), loaded_plain(wx0a), woven_plain(both0[0][:, 0:SPAN]), ALU.subtract
         )
         x0 = [load_piece(x, 0, "x0" + "ab"[h], h * HALF, HALF) for h in range(2)]
         wx0b = load_piece(wx, 0, "wx0b", HALF, HALF)
         move_scales(1, picked1)
-        load_columns(1, JT - 1)
         load_columns(2, 0)
         wx1 = [load_piece(wx, 1, "wx1" + "ab"[h], h * HALF, HALF) for h in range(2)]
         load_columns(3, 0)
@@ -175,7 +178,7 @@ def tile_list_interp_hl_res_kernel(
         nc.gpsimd.tensor_scalar(woven_plain(rounded0a[:]), loaded_plain(x0[0]), 1.0, 0.0, ALU.mult, ALU.add)
 
         q_wx, q_x = {}, {}
-        rest0 = sbuf([P, 2 * SPAN], BF16, "rest0", after="upper0a")
+        rest0 = placed([P, 2 * SPAN], BF16, "rest0", 0)
         upper0b, rounded0b = rest0[:, 0:SPAN], rest0[:, SPAN : 2 * SPAN]
         nc.vector.tensor_copy(woven(upper0b), loaded(tops(wx0b)))
         nc.vector.tensor_copy(woven(rounded0b), loaded(x0[1]))
@@ -202,7 +205,10 @@ def tile_list_interp_hl_res_kernel(
                     lhsT_scale=got_s[:, g * J + jt * P : g * J + (jt + 1) * P],
                     rhs=w_w[:].bitcast(FP4X4), rhs_scale=w_s[:], start=True, stop=True,
                 )
-                parts[g, jt] = sbuf([P, N], F32, f"part{g}_{jt}")
+                if (g, jt) == (1, JT - 1):
+                    parts[g, jt] = placed([P, N], F32, f"part{g}_{jt}", 4 * SPAN)
+                else:
+                    parts[g, jt] = sbuf([P, N], F32, f"part{g}_{jt}")
                 nc.scalar.activation(parts[g, jt][:], acc[:], COPY, scale=scale_of[g, jt])
                 if g == 1 and jt % 2 == 1:
                     add_transposed(0, (jt, jt - 1))

@@ -28,6 +28,11 @@ FIRST_ROW = P - 16
 LIST_ROWS = 16
 RUN = 2
 BLOCK = 8
+LINE = 64
+EARLY = 7 * T // 8
+WARM = 3
+LATE = 8 * SPAN
+SHARE = 96
 HI_MASK = 0xFFF0FFF0 - (1 << 32)
 
 
@@ -75,7 +80,7 @@ def tile_list_interp_hl_res_kernel(
         w_s = sbuf([P, N], U8, "w_s")
         ident = sbuf([P, P], F32, "ident")
         iw_rows = sbuf([P, P], F32, "iw_rows")
-        iw_cols = sbuf([P, 2 * JT], F32, "iw_cols")
+        iw_cols = sbuf([P, (G - 1) * JT], F32, "iw_cols")
         got_s = sbuf([P, G * J], U8, "got_s")
         weights = (iw0, iw1, iw2, iw3)
         scale_of = {}
@@ -93,8 +98,10 @@ def tile_list_interp_hl_res_kernel(
             for jt in range(first, JT):
                 scale_of[g, jt] = cols[:, jt - first, 0:1]
 
-        def load_piece(src, a, name, first, width):
-            raw = sbuf([P, PACK * width], F32, name)[:].rearrange("p (t c) -> p t c", t=PACK)
+        def load_piece(src, a, name, first, width, offset=None):
+            shape = [P, PACK * width]
+            tile = sbuf(shape, F32, name) if offset is None else placed(shape, F32, name, offset)
+            raw = tile[:].rearrange("p (t c) -> p t c", t=PACK)
             rows = src[a * P * PACK : (a + 1) * P * PACK, first : first + width]
             nc.sync.dma_start(raw, rows.rearrange("(p t) c -> p t c", t=PACK))
             return raw
@@ -140,33 +147,41 @@ def tile_list_interp_hl_res_kernel(
         for q in range(4):
             nc.vector.tensor_copy(as_int32(w_s)[q * QUAD : q * QUAD + 4, :], w_rows[:, q, :])
         wx0a = load_piece(wx, 0, "wx0a", 0, HALF)
-        load_rows(0, JT)
-        load_rows(1, JT)
-        nc.sync.dma_start(as_int32(tab_w), tab_words[0].rearrange("p t i -> p (t i)").bitcast(I32))
-        nc.sync.dma_start(as_int32(w_w), w_words[0].bitcast(I32))
+        for g in range(G - 1):
+            load_rows(g, JT)
+        table = tab_words[0].rearrange("p t i -> p (t i)").bitcast(I32)
+        nc.sync.dma_start(as_int32(tab_w)[:, 0:EARLY], table[:, 0:EARLY])
 
         both0 = [sbuf([P, 2 * SPAN], BF16, "both0" + "ab"[h]) for h in range(2)]
-        upper0a = placed([P, SPAN], BF16, "upper0a", 2 * SPAN)
+        upper0a = placed([P, SPAN], BF16, "upper0a", SPAN)
         nc.scalar.copy(woven(upper0a[:]), loaded(tops(wx0a)))
         iw_turned = bank(JT - 1, "iw_turned")
         nc.tensor.transpose(iw_turned[:, 0:P], iw_rows[:], ident[:])
-        nc.scalar.activation(iw_cols[:], iw_turned[:, 0 : 2 * JT], COPY)
+        nc.scalar.activation(iw_cols[:], iw_turned[:, 0 : (G - 1) * JT], COPY)
+
+        warm = bank(0, "warm")
+        for step in range(WARM):
+            nc.tensor.matmul_mx(
+                warm[:], lhsT=tab_w[:, step * P : (step + 1) * P].bitcast(FP8X4), lhsT_scale=w_s[:, 0:P],
+                rhs=tab_w[:, 0:N].bitcast(FP8X4), rhs_scale=w_s[:], start=True, stop=True,
+            )
 
         move_scales(0, gather_scales(0, sbuf([P, 2 * J], U8, "picked0")))
+        nc.sync.dma_start(as_int32(tab_w)[:, EARLY:T], table[:, EARLY:T])
+        nc.sync.dma_start(as_int32(w_w), w_words[0].bitcast(I32))
         truncate(upper0a[:], both0[0][:, 0:SPAN])
-        picked1 = gather_scales(1, placed([P, 2 * J], U8, "picked1", 4 * SPAN - J))
+        picked1 = gather_scales(1, placed([P, 2 * J], U8, "picked1", 2 * SPAN - LINE))
         nc.gpsimd.tensor_tensor(
             woven_plain(both0[0][:, SPAN : 2 * SPAN]), loaded_plain(wx0a), woven_plain(both0[0][:, 0:SPAN]), ALU.subtract
         )
         x0 = [load_piece(x, 0, "x0" + "ab"[h], h * HALF, HALF) for h in range(2)]
         wx0b = load_piece(wx, 0, "wx0b", HALF, HALF)
         move_scales(1, picked1)
-        load_columns(2, 0)
         wx1 = [load_piece(wx, 1, "wx1" + "ab"[h], h * HALF, HALF) for h in range(2)]
-        load_columns(3, 0)
-        x1 = load_piece(x, 1, "x1", 0, J)
         res_sb = sbuf([P, NT, J], F32, "res_sb")
         nc.sync.dma_start(res_sb[:], res.rearrange("(nt p) j -> p nt j", p=P))
+        load_columns(3, 0)
+        x1 = load_piece(x, 1, "x1", 0, J, LATE)
 
         got_w = {}
         for g in range(G):
@@ -174,27 +189,28 @@ def tile_list_interp_hl_res_kernel(
             entries = offsets[:, g * J // LIST_ROWS : (g + 1) * J // LIST_ROWS]
             nc.vector.tensor_copy(got_w[g][:], tab_w[:].indirect(entries))
 
-        rounded0a = sbuf([P, SPAN], BF16, "rounded0a")
-        nc.gpsimd.tensor_scalar(woven_plain(rounded0a[:]), loaded_plain(x0[0]), 1.0, 0.0, ALU.mult, ALU.add)
+        rounded0 = [sbuf([P, SPAN], BF16, "rounded0" + "ab"[h]) for h in range(2)]
+        for h in range(2):
+            nc.gpsimd.tensor_scalar(woven_plain(rounded0[h][:]), loaded_plain(x0[h]), 1.0, 0.0, ALU.mult, ALU.add)
 
         q_wx, q_x = {}, {}
-        rest0 = placed([P, 2 * SPAN], BF16, "rest0", 0)
-        upper0b, rounded0b = rest0[:, 0:SPAN], rest0[:, SPAN : 2 * SPAN]
-        nc.vector.tensor_copy(woven(upper0b), loaded(tops(wx0b)))
-        nc.vector.tensor_copy(woven(rounded0b), loaded(x0[1]))
-        truncate(upper0b, both0[1][:, 0:SPAN])
-        q_wx[0, 0] = quantise(both0[0][:], "q_wx0a", after="x0b")
+        upper0b = placed([P, SPAN], BF16, "upper0b", 0)
+        nc.vector.tensor_copy(woven(upper0b[:]), loaded(tops(wx0b)))
+        q_wx[0, 0] = sbuf([P, N], U32, "q_wx0a_codes"), placed([P, N], U8, "q_wx0a_scales", 2 * SPAN + LINE)
+        quantise_into(q_wx[0, 0], 0, both0[0][:, 0:SPAN])
+        truncate(upper0b[:], both0[1][:, 0:SPAN])
+        quantise_into(q_wx[0, 0], HALF, both0[0][:, SPAN:])
         subtract(wx0b, both0[1][:])
 
         sums = [psum.tile([P, J], F32, name=f"sum{nt}") for nt in range(NT)]
         parts = {}
 
-        def add_transposed(g, tiles, rows=range(NT)):
-            for jt in tiles:
+        def add_transposed(run, rows=range(NT)):
+            for g, jt in run:
                 for nt in rows:
                     nc.tensor.matmul(
                         sums[nt][:, jt * P : (jt + 1) * P], parts[g, jt][:, nt * P : (nt + 1) * P], ident[:],
-                        start=(g, jt) == (0, 1), stop=(g, jt) == (G - 1, JT - 2), is_transpose=True,
+                        start=(g, jt) == (0, 1), stop=(g, jt) == (G - 1, 0), is_transpose=True,
                     )
 
         for g in range(G):
@@ -206,33 +222,36 @@ def tile_list_interp_hl_res_kernel(
                     rhs=w_w[:].bitcast(FP4X4), rhs_scale=w_s[:], start=True, stop=True,
                 )
                 if (g, jt) == (1, JT - 1):
-                    parts[g, jt] = placed([P, N], F32, f"part{g}_{jt}", 4 * SPAN)
+                    parts[g, jt] = placed([P, N], F32, f"part{g}_{jt}", 2 * SPAN + 2 * J - 2 * LINE)
                 else:
                     parts[g, jt] = sbuf([P, N], F32, f"part{g}_{jt}")
                 nc.scalar.activation(parts[g, jt][:], acc[:], COPY, scale=scale_of[g, jt])
-                if g == 1 and jt % 2 == 1:
-                    add_transposed(0, (jt, jt - 1))
-            if g > 1:
-                add_transposed(g - 1, reversed(range(JT)))
-        rounded1 = sbuf([P, 2 * SPAN], BF16, "rounded1", after="got_w2")
+                if (g, jt) == (1, 1):
+                    add_transposed([(0, 1), (0, 0)])
+            if g == 1:
+                add_transposed([(0, 3), (0, 2), (1, 0)])
+            if g == 2:
+                add_transposed([(1, 3), (1, 2), (1, 1)])
+                upper1b = sbuf([P, SPAN], BF16, "upper1b", after="got_w1")
+                nc.scalar.copy(woven(upper1b[:, SHARE * PACK :]), loaded(tops(wx1[1][:, :, SHARE:])))
+        add_transposed([(2, jt) for jt in reversed(range(JT))])
+        rounded1 = sbuf([P, 2 * SPAN], BF16, "rounded1", after="got_w3")
         nc.scalar.copy(woven(rounded1[:]), loaded(x1))
 
-        upper1 = sbuf([P, 2 * SPAN], BF16, "upper1")
-        both1 = sbuf([P, 4 * SPAN], BF16, "both1")
-        nc.vector.tensor_copy(woven(upper1[:, 0:SPAN]), loaded(tops(wx1[0])))
-        q_wx[1, 0] = quantise(both0[1][:], "q_wx0b", after="part1_0")
-        nc.vector.tensor_copy(woven(upper1[:, SPAN : 2 * SPAN]), loaded(tops(wx1[1])))
-        q_x[0] = coded(J, "q_x0", after="both0b")
-        quantise_into(q_x[0], 0, rounded0a[:])
-        truncate(
-            upper1[:].rearrange("p (h e) -> p h e", h=2), both1[:].rearrange("p (h s e) -> p h s e", h=2, s=2)[:, :, 0, :]
-        )
-        quantise_into(q_x[0], HALF, rounded0b)
+        both1 = [sbuf([P, 2 * SPAN], BF16, "both1" + "ab"[h]) for h in range(2)]
+        upper1a = sbuf([P, SPAN], BF16, "upper1a")
+        nc.vector.tensor_copy(woven(upper1a[:]), loaded(tops(wx1[0])))
+        q_x[0] = coded(J, "q_x0", after="both0a")
+        quantise_into(q_x[0], 0, rounded0[0][:])
+        truncate(upper1a[:], both1[0][:, 0:SPAN])
+        nc.vector.tensor_copy(woven(upper1b[:, 0 : SHARE * PACK]), loaded(tops(wx1[1][:, :, 0:SHARE])))
+        quantise_into(q_x[0], HALF, rounded0[1][:])
+        subtract(wx1[0], both1[0][:])
+        truncate(upper1b[:], both1[1][:, 0:SPAN])
+        q_wx[1, 0] = quantise(both0[1][:], "q_wx0b", after="rounded0a")
+        subtract(wx1[1], both1[1][:])
         for h in range(2):
-            subtract(wx1[h], both1[:, 2 * h * SPAN : 2 * (h + 1) * SPAN])
-        for h in range(2):
-            q_wx[h, 1] = quantise(both1[:, 2 * h * SPAN : 2 * (h + 1) * SPAN], "q_wx1" + "ab"[h])
-        q_x[1] = quantise(rounded1[:], "q_x1")
+            q_wx[h, 1] = quantise(both1[h][:], "q_wx1" + "ab"[h])
 
         skip = [bank(nt, f"skip{nt}") for nt in range(NT)]
 
@@ -247,19 +266,20 @@ def tile_list_interp_hl_res_kernel(
                 )
 
         skip_pass(0, 0)
-        add_transposed(G - 1, (1, 0))
         skip_pass(1, 0)
-        for nt in (2, 3, 0, 1):
-            add_transposed(G - 1, (3, 2), rows=[nt])
+        for nt in (0, 2, 3, 1):
+            add_transposed([(G - 1, jt) for jt in reversed(range(JT))], rows=[nt])
         skip_pass(2, 0)
         skip_pass(3, 0)
 
-        bases = sbuf([P, NT * J], F32, "bases", after="got_w2")
-        base = [bases[:, nt * J : (nt + 1) * J] for nt in range(NT)]
-        moved = sbuf([P, NT // 2 * J], F32, "moved", after="x1")
+        first = sbuf([P, J], F32, "base0", after="both1a")
+        bases = sbuf([P, (NT - 1) * J], F32, "bases", after="got_w3")
+        base = [first[:]] + [bases[:, nt * J : (nt + 1) * J] for nt in range(NT - 1)]
+        moved = placed([P, NT // 2 * J], F32, "moved", LATE)
         done = sbuf([P, NT * J], F32, "done")
-        for nt in range(NT // 2):
-            nc.vector.tensor_tensor(base[nt], sums[nt][:], res_sb[:, nt, :], ALU.add)
+        nc.vector.tensor_tensor(base[0], sums[0][:], res_sb[:, 0, :], ALU.add)
+        q_x[1] = quantise(rounded1[:], "q_x1")
+        nc.vector.tensor_tensor(base[1], sums[1][:], res_sb[:, 1, :], ALU.add)
         for nt in range(NT // 2, NT):
             copied = moved[:, (nt - NT // 2) * J : (nt - NT // 2 + 1) * J]
             nc.scalar.copy(copied, sums[nt][:])

@@ -186,8 +186,10 @@ def tile_list_interp_hl_res_kernel(
         got_w = {}
         for g in range(G):
             got_w[g] = sbuf([P, J], U32, f"got_w{g}")
-            entries = offsets[:, g * J // LIST_ROWS : (g + 1) * J // LIST_ROWS]
-            nc.vector.tensor_copy(got_w[g][:], tab_w[:].indirect(entries))
+            width = J // 2 if g == 0 else J
+            for first in range(0, J, width):
+                entries = offsets[:, (g * J + first) // LIST_ROWS : (g * J + first + width) // LIST_ROWS]
+                nc.vector.tensor_copy(got_w[g][:, first : first + width], tab_w[:].indirect(entries))
 
         rounded0 = [sbuf([P, SPAN], BF16, "rounded0" + "ab"[h]) for h in range(2)]
         for h in range(2):

@@ -30,7 +30,6 @@ RUN = 2
 BLOCK = 8
 LINE = 64
 EARLY = 7 * T // 8
-WARM = 3
 LATE = 8 * SPAN
 SHARE = 96
 HI_MASK = 0xFFF0FFF0 - (1 << 32)
@@ -158,13 +157,6 @@ def tile_list_interp_hl_res_kernel(
         iw_turned = bank(JT - 1, "iw_turned")
         nc.tensor.transpose(iw_turned[:, 0:P], iw_rows[:], ident[:])
         nc.scalar.activation(iw_cols[:], iw_turned[:, 0 : (G - 1) * JT], COPY)
-
-        warm = bank(0, "warm")
-        for step in range(WARM):
-            nc.tensor.matmul_mx(
-                warm[:], lhsT=tab_w[:, step * P : (step + 1) * P].bitcast(FP8X4), lhsT_scale=w_s[:, 0:P],
-                rhs=tab_w[:, 0:N].bitcast(FP8X4), rhs_scale=w_s[:], start=True, stop=True,
-            )
 
         move_scales(0, gather_scales(0, sbuf([P, 2 * J], U8, "picked0")))
         nc.sync.dma_start(as_int32(tab_w)[:, EARLY:T], table[:, EARLY:T])

@@ -31,7 +31,7 @@ BLOCK = 8
 LINE = 64
 EARLY = 7 * T // 8
 LATE = 8 * SPAN
-SHARE = 96
+SHARE = 64
 HI_MASK = 0xFFF0FFF0 - (1 << 32)
 
 
@@ -204,7 +204,7 @@ def tile_list_interp_hl_res_kernel(
                 for nt in rows:
                     nc.tensor.matmul(
                         sums[nt][:, jt * P : (jt + 1) * P], parts[g, jt][:, nt * P : (nt + 1) * P], ident[:],
-                        start=(g, jt) == (0, 1), stop=(g, jt) == (G - 1, 0), is_transpose=True,
+                        start=(g, jt) == (0, 3), stop=(g, jt) == (3, 1), is_transpose=True,
                     )
 
         for g in range(G):
@@ -220,15 +220,15 @@ def tile_list_interp_hl_res_kernel(
                 else:
                     parts[g, jt] = sbuf([P, N], F32, f"part{g}_{jt}")
                 nc.scalar.activation(parts[g, jt][:], acc[:], COPY, scale=scale_of[g, jt])
-                if (g, jt) == (1, 1):
-                    add_transposed([(0, 1), (0, 0)])
             if g == 1:
-                add_transposed([(0, 3), (0, 2), (1, 0)])
+                add_transposed([(0, 3), (0, 2), (0, 1)])
             if g == 2:
-                add_transposed([(1, 3), (1, 2), (1, 1)])
+                add_transposed([(1, 3), (0, 0), (1, 0)])
+                add_transposed([(1, 1)], rows=(0, 1))
                 upper1b = sbuf([P, SPAN], BF16, "upper1b", after="got_w1")
                 nc.scalar.copy(woven(upper1b[:, SHARE * PACK :]), loaded(tops(wx1[1][:, :, SHARE:])))
-        add_transposed([(2, jt) for jt in reversed(range(JT))])
+        add_transposed([(2, 3), (1, 2), (2, 0)])
+        add_transposed([(1, 1)], rows=(2, 3))
         rounded1 = sbuf([P, 2 * SPAN], BF16, "rounded1", after="got_w3")
         nc.scalar.copy(woven(rounded1[:]), loaded(x1))
 
@@ -260,20 +260,20 @@ def tile_list_interp_hl_res_kernel(
                 )
 
         skip_pass(0, 0)
+        add_transposed([(3, 0), (2, 1), (2, 2)])
         skip_pass(1, 0)
-        for nt in (0, 2, 3, 1):
-            add_transposed([(G - 1, jt) for jt in reversed(range(JT))], rows=[nt])
+        for nt in (2, 3, 0, 1):
+            add_transposed([(3, 3), (3, 2), (3, 1)], rows=[nt])
         skip_pass(2, 0)
         skip_pass(3, 0)
 
-        first = sbuf([P, J], F32, "base0", after="both1a")
-        bases = sbuf([P, (NT - 1) * J], F32, "bases", after="got_w3")
-        base = [first[:]] + [bases[:, nt * J : (nt + 1) * J] for nt in range(NT - 1)]
+        bases = sbuf([P, NT * J], F32, "bases", after="got_w3")
+        base = [bases[:, nt * J : (nt + 1) * J] for nt in range(NT)]
         moved = placed([P, NT // 2 * J], F32, "moved", LATE)
         done = sbuf([P, NT * J], F32, "done")
-        nc.vector.tensor_tensor(base[0], sums[0][:], res_sb[:, 0, :], ALU.add)
         q_x[1] = quantise(rounded1[:], "q_x1")
-        nc.vector.tensor_tensor(base[1], sums[1][:], res_sb[:, 1, :], ALU.add)
+        for nt in range(NT // 2):
+            nc.vector.tensor_tensor(base[nt], sums[nt][:], res_sb[:, nt, :], ALU.add)
         for nt in range(NT // 2, NT):
             copied = moved[:, (nt - NT // 2) * J : (nt - NT // 2 + 1) * J]
             nc.scalar.copy(copied, sums[nt][:])

@@ -170,10 +170,10 @@ def tile_list_interp_hl_res_kernel(
         wx0b = load_piece(wx, 0, "wx0b", HALF, HALF)
         move_scales(1, picked1)
         wx1 = [load_piece(wx, 1, "wx1" + "ab"[h], h * HALF, HALF) for h in range(2)]
-        res_sb = sbuf([P, NT, J], F32, "res_sb")
-        nc.sync.dma_start(res_sb[:], res.rearrange("(nt p) j -> p nt j", p=P))
         load_columns(3, 0)
         x1 = load_piece(x, 1, "x1", 0, J, LATE)
+        res_sb = sbuf([P, NT, J], F32, "res_sb")
+        nc.sync.dma_start(res_sb[:], res.rearrange("(nt p) j -> p nt j", p=P))
 
         got_w = {}
         for g in range(G):

from contextlib import ExitStack

import concourse.mybir as mybir
from concourse.masks import make_identity

K, L, N, T, J, G = 512, 1024, 512, 4096, 512, 4
FLOPS = 2 * N * J * (G * K + 2 * L)

F32 = mybir.dt.float32
BF16 = mybir.dt.bfloat16
I32 = mybir.dt.int32
U32 = mybir.dt.uint32
U16 = mybir.dt.uint16
U8 = mybir.dt.uint8
FP8X4 = mybir.dt.float8_e4m3fn_x4
FP4X4 = mybir.dt.float4_e2m1fn_x4
ALU = mybir.AluOpType
COPY = mybir.ActivationFunctionType.Copy

P = 128
PACK = 4
JT = J // P
NT = N // P
HALF = N // 2
SPAN = HALF * PACK
QUAD = 32
FIRST_ROW = P - 16
LIST_ROWS = 16
RUN = 2
BLOCK = 8
LINE = 64
EARLY = 7 * T // 8
LATE = 8 * SPAN
SHARE = 64
HI_MASK = 0xFFF0FFF0 - (1 << 32)


def tile_list_interp_hl_res_kernel(
    tc, tab_words, tab_scales, w_words, w_scales, x, wx, iw0, iw1, iw2, iw3, res, offs, out
):
    nc = tc.nc

    def as_int32(tile):
        return tile[:].bitcast(I32)

    def loaded(raw):
        return raw.rearrange("p t (c i) -> p c t i", i=RUN)

    def woven(run):
        return run.rearrange("p (c i t) -> p c t i", i=RUN, t=PACK)

    def loaded_plain(raw):
        return raw.rearrange("p t c -> p c t")

    def woven_plain(run):
        return run.rearrange("p (c t) -> p c t", t=PACK)

    def tops(raw):
        return raw.bitcast(BF16).rearrange("p t (c two) -> p t c two", two=2)[:, :, :, 1]

    with ExitStack() as ctx:
        held = ctx.enter_context(tc.tile_pool(name="held", bufs=1))
        laid = ctx.enter_context(tc.tile_pool(name="laid", bufs=1))
        psum = ctx.enter_context(tc.psum_pool(name="psum", bufs=1))

        def placed(shape, dtype, name, offset):
            return laid.tile(shape, dtype, name=name, offset=offset, align_bytes=64)

        def sbuf(shape, dtype, name, after=None):
            return held.tile(shape, dtype, name=name, tag=after or name, align_bytes=64)

        def bank(b, name):
            return psum.tile([P, N], F32, name=name, tag=f"bank{b}")

        offsets = held.tile([P, G * J // LIST_ROWS], U16, name="offsets")
        tab_s = sbuf([P, T], U8, "tab_s")
        tab_w = sbuf([P, T], U32, "tab_w")
        w_w = sbuf([P, 2 * N], U8, "w_w")
        w_s = sbuf([P, N], U8, "w_s")
        ident = sbuf([P, P], F32, "ident")
        iw_rows = sbuf([P, P], F32, "iw_rows")
        iw_cols = sbuf([P, (G - 1) * JT], F32, "iw_cols")
        got_s = sbuf([P, G * J], U8, "got_s")
        weights = (iw0, iw1, iw2, iw3)
        scale_of = {}

        def load_rows(g, count):
            rows = weights[g].rearrange("(jt p) -> jt p", p=P)
            nc.sync.dma_start(iw_rows[g * JT : g * JT + count, :], rows[0:count, :])
            for jt in range(count):
                scale_of[g, jt] = iw_cols[:, g * JT + jt : g * JT + jt + 1]

        def load_columns(g, first):
            cols = sbuf([P, JT - first, BLOCK], F32, f"iw_cols{g}")
            with nc.allow_non_contiguous_dma(reason="one weight a partition and tile"):
                nc.sync.dma_start(cols[:, :, 0], weights[g].rearrange("(jt p) -> p jt", p=P)[:, first:JT])
            for jt in range(first, JT):
                scale_of[g, jt] = cols[:, jt - first, 0:1]

        def load_piece(src, a, name, first, width, offset=None):
            shape = [P, PACK * width]
            tile = sbuf(shape, F32, name) if offset is None else placed(shape, F32, name, offset)
            raw = tile[:].rearrange("p (t c) -> p t c", t=PACK)
            rows = src[a * P * PACK : (a + 1) * P * PACK, first : first + width]
            nc.sync.dma_start(raw, rows.rearrange("(p t) c -> p t c", t=PACK))
            return raw

        def gather_scales(h, picked):
            entries = offsets[:, 2 * h * J // LIST_ROWS : 2 * (h + 1) * J // LIST_ROWS]
            nc.vector.tensor_copy(picked[:], tab_s[:].indirect(entries))
            return picked

        def move_scales(h, picked):
            plane = as_int32(got_s)[:, h * J // 2 : (h + 1) * J // 2]
            for r in range(4):
                nc.sync.dma_start(plane[r:P:QUAD, :], as_int32(picked)[FIRST_ROW + r : P : 4, :])

        def truncate(upper, hi):
            nc.vector.tensor_scalar(hi.bitcast(I32), upper.bitcast(I32), HI_MASK, None, ALU.bitwise_and)

        def subtract(raw, both):
            nc.vector.tensor_tensor(woven(both[:, SPAN : 2 * SPAN]), loaded(raw), woven(both[:, 0:SPAN]), ALU.subtract)

        def coded(width, name, after=None):
            return sbuf([P, width], U32, name + "_codes", after), sbuf([P, width], U8, name + "_scales")

        def quantise_into(target, first, src):
            cols = slice(first, first + src.shape[1] // PACK)
            nc.vector.quantize_mx(out=target[0][:, cols].bitcast(FP8X4), scales=target[1][:, cols], in_=src)

        def quantise(src, name, after=None):
            target = coded(src.shape[1] // PACK, name, after)
            quantise_into(target, 0, src)
            return target

        nc.gpsimd.memset(iw_rows[:], 0.0)
        nc.gpsimd.memset(as_int32(tab_s)[0:FIRST_ROW, 0 : T // 8], 0)
        make_identity(nc, ident[:])
        nc.vector.memset(as_int32(w_s), 0)
        nc.vector.memset(as_int32(tab_s)[0:FIRST_ROW, T // 8 : T // 4], 0)
        nc.vector.memset(as_int32(got_s), 0)
        w_rows = sbuf([4, 4, N // 4], I32, "w_rows")
        nc.sync.dma_start(w_rows[:], w_scales[0].bitcast(I32).rearrange("(q r) c -> r q c", r=4))
        nc.sync.dma_start(as_int32(tab_s)[FIRST_ROW:P, :], tab_scales[0].bitcast(I32))
        nc.sync.dma_start(offsets[:], offs)
        for q in range(4):
            nc.vector.tensor_copy(as_int32(w_s)[q * QUAD : q * QUAD + 4, :], w_rows[:, q, :])
        wx0a = load_piece(wx, 0, "wx0a", 0, HALF)
        for g in range(G - 1):
            load_rows(g, JT)
        table = tab_words[0].rearrange("p t i -> p (t i)").bitcast(I32)
        nc.sync.dma_start(as_int32(tab_w)[:, 0:EARLY], table[:, 0:EARLY])

        both0 = [sbuf([P, 2 * SPAN], BF16, "both0" + "ab"[h]) for h in range(2)]
        upper0a = placed([P, SPAN], BF16, "upper0a", SPAN)
        nc.scalar.copy(woven(upper0a[:]), loaded(tops(wx0a)))
        iw_turned = bank(JT - 1, "iw_turned")
        nc.tensor.transpose(iw_turned[:, 0:P], iw_rows[:], ident[:])
        nc.scalar.activation(iw_cols[:], iw_turned[:, 0 : (G - 1) * JT], COPY)

        move_scales(0, gather_scales(0, sbuf([P, 2 * J], U8, "picked0")))
        nc.sync.dma_start(as_int32(tab_w)[:, EARLY:T], table[:, EARLY:T])
        nc.sync.dma_start(as_int32(w_w), w_words[0].bitcast(I32))
        truncate(upper0a[:], both0[0][:, 0:SPAN])
        picked1 = gather_scales(1, placed([P, 2 * J], U8, "picked1", 2 * SPAN - LINE))
        nc.gpsimd.tensor_tensor(
            woven_plain(both0[0][:, SPAN : 2 * SPAN]), loaded_plain(wx0a), woven_plain(both0[0][:, 0:SPAN]), ALU.subtract
        )
        x0 = [load_piece(x, 0, "x0" + "ab"[h], h * HALF, HALF) for h in range(2)]
        wx0b = load_piece(wx, 0, "wx0b", HALF, HALF)
        move_scales(1, picked1)
        wx1 = [load_piece(wx, 1, "wx1" + "ab"[h], h * HALF, HALF) for h in range(2)]
        load_columns(3, 0)
        x1 = load_piece(x, 1, "x1", 0, J, LATE)
        res_sb = sbuf([P, NT, J], F32, "res_sb")
        nc.sync.dma_start(res_sb[:], res.rearrange("(nt p) j -> p nt j", p=P))

        got_w = {}
        for g in range(G):
            got_w[g] = sbuf([P, J], U32, f"got_w{g}")
            width = J // 2 if g == 0 else J
            for first in range(0, J, width):
                entries = offsets[:, (g * J + first) // LIST_ROWS : (g * J + first + width) // LIST_ROWS]
                nc.vector.tensor_copy(got_w[g][:, first : first + width], tab_w[:].indirect(entries))

        rounded0 = [sbuf([P, SPAN], BF16, "rounded0" + "ab"[h]) for h in range(2)]
        for h in range(2):
            nc.gpsimd.tensor_scalar(woven_plain(rounded0[h][:]), loaded_plain(x0[h]), 1.0, 0.0, ALU.mult, ALU.add)

        q_wx, q_x = {}, {}
        upper0b = placed([P, SPAN], BF16, "upper0b", 0)
        nc.vector.tensor_copy(woven(upper0b[:]), loaded(tops(wx0b)))
        q_wx[0, 0] = sbuf([P, N], U32, "q_wx0a_codes"), placed([P, N], U8, "q_wx0a_scales", 2 * SPAN + LINE)
        quantise_into(q_wx[0, 0], 0, both0[0][:, 0:SPAN])
        truncate(upper0b[:], both0[1][:, 0:SPAN])
        quantise_into(q_wx[0, 0], HALF, both0[0][:, SPAN:])
        subtract(wx0b, both0[1][:])

        sums = [psum.tile([P, J], F32, name=f"sum{nt}") for nt in range(NT)]
        parts = {}

        def add_transposed(run, rows=range(NT)):
            for g, jt in run:
                for nt in rows:
                    nc.tensor.matmul(
                        sums[nt][:, jt * P : (jt + 1) * P], parts[g, jt][:, nt * P : (nt + 1) * P], ident[:],
                        start=(g, jt) == (0, 3), stop=(g, jt) == (3, 1), is_transpose=True,
                    )

        for g in range(G):
            for jt in range(JT):
                acc = bank(jt, f"acc{g}_{jt}")
                nc.tensor.matmul_mx(
                    acc[:], lhsT=got_w[g][:, jt * P : (jt + 1) * P].bitcast(FP8X4),
                    lhsT_scale=got_s[:, g * J + jt * P : g * J + (jt + 1) * P],
                    rhs=w_w[:].bitcast(FP4X4), rhs_scale=w_s[:], start=True, stop=True,
                )
                if (g, jt) == (1, JT - 1):
                    parts[g, jt] = placed([P, N], F32, f"part{g}_{jt}", 2 * SPAN + 2 * J - 2 * LINE)
                else:
                    parts[g, jt] = sbuf([P, N], F32, f"part{g}_{jt}")
                nc.scalar.activation(parts[g, jt][:], acc[:], COPY, scale=scale_of[g, jt])
            if g == 1:
                add_transposed([(0, 3), (0, 2), (0, 1)])
            if g == 2:
                add_transposed([(1, 3), (0, 0), (1, 0)])
                add_transposed([(1, 1)], rows=(0, 1))
                upper1b = sbuf([P, SPAN], BF16, "upper1b", after="got_w1")
                nc.scalar.copy(woven(upper1b[:, SHARE * PACK :]), loaded(tops(wx1[1][:, :, SHARE:])))
        add_transposed([(2, 3), (1, 2), (2, 0)])
        add_transposed([(1, 1)], rows=(2, 3))
        rounded1 = sbuf([P, 2 * SPAN], BF16, "rounded1", after="got_w3")
        nc.scalar.copy(woven(rounded1[:]), loaded(x1))

        both1 = [sbuf([P, 2 * SPAN], BF16, "both1" + "ab"[h]) for h in range(2)]
        upper1a = sbuf([P, SPAN], BF16, "upper1a")
        nc.vector.tensor_copy(woven(upper1a[:]), loaded(tops(wx1[0])))
        q_x[0] = coded(J, "q_x0", after="both0a")
        quantise_into(q_x[0], 0, rounded0[0][:])
        truncate(upper1a[:], both1[0][:, 0:SPAN])
        nc.vector.tensor_copy(woven(upper1b[:, 0 : SHARE * PACK]), loaded(tops(wx1[1][:, :, 0:SHARE])))
        quantise_into(q_x[0], HALF, rounded0[1][:])
        subtract(wx1[0], both1[0][:])
        truncate(upper1b[:], both1[1][:, 0:SPAN])
        q_wx[1, 0] = quantise(both0[1][:], "q_wx0b", after="rounded0a")
        subtract(wx1[1], both1[1][:])
        for h in range(2):
            q_wx[h, 1] = quantise(both1[h][:], "q_wx1" + "ab"[h])

        skip = [bank(nt, f"skip{nt}") for nt in range(NT)]

        def skip_pass(nt, a):
            codes, scales = q_wx[nt // 2, a]
            for s in range(2):
                cols = slice(s * HALF + nt % 2 * P, s * HALF + (nt % 2 + 1) * P)
                nc.tensor.matmul_mx(
                    skip[nt][:], lhsT=codes[:, cols].bitcast(FP8X4), lhsT_scale=scales[:, cols],
                    rhs=q_x[a][0][:].bitcast(FP8X4), rhs_scale=q_x[a][1][:],
                    start=a == 0 and s == 0, stop=a == 1 and s == 1,
                )

        skip_pass(0, 0)
        add_transposed([(3, 0), (2, 1), (2, 2)])
        skip_pass(1, 0)
        for nt in (2, 3, 0, 1):
            add_transposed([(3, 3), (3, 2), (3, 1)], rows=[nt])
        skip_pass(2, 0)
        skip_pass(3, 0)

        bases = sbuf([P, NT * J], F32, "bases", after="got_w3")
        base = [bases[:, nt * J : (nt + 1) * J] for nt in range(NT)]
        moved = placed([P, NT // 2 * J], F32, "moved", LATE)
        done = sbuf([P, NT * J], F32, "done")
        q_x[1] = quantise(rounded1[:], "q_x1")
        for nt in range(NT // 2):
            nc.vector.tensor_tensor(base[nt], sums[nt][:], res_sb[:, nt, :], ALU.add)
        for nt in range(NT // 2, NT):
            copied = moved[:, (nt - NT // 2) * J : (nt - NT // 2 + 1) * J]
            nc.scalar.copy(copied, sums[nt][:])
            pieces = 2 if nt == NT - 1 else 1
            for piece in range(pieces):
                part = slice(piece * J // pieces, (piece + 1) * J // pieces)
                nc.gpsimd.tensor_tensor(base[nt][:, part], copied[:, part], res_sb[:, nt, part], ALU.add)

        for nt in range(NT):
            skip_pass(nt, 1)
        for nt in range(NT):
            pieces = 2 if nt == NT - 1 else 1
            for piece in range(pieces):
                cols = slice(piece * J // pieces, (piece + 1) * J // pieces)
                place = slice(nt * J + cols.start, nt * J + cols.stop)
                nc.vector.tensor_tensor(done[:, place], skip[nt][:, cols], base[nt][:, cols], ALU.add)
                nc.sync.dma_start(out[nt * P : (nt + 1) * P, cols], done[:, place])
